import numpy as np
import ml_dtypes


def mxq(x, axis, fmt="e4m3"):
    dtype, down = {"e4m3": (ml_dtypes.float8_e4m3fn, 7), "e5m2": (ml_dtypes.float8_e5m2, 14)}[fmt]
    v = np.moveaxis(np.asarray(x, np.float32).astype(ml_dtypes.bfloat16).astype(np.float64), axis, -1)
    blocks = v.reshape(v.shape[:-1] + (-1, 32))
    amax = np.abs(blocks).max(-1, keepdims=True)
    byte = np.maximum(np.where(amax > 0, np.frexp(amax)[1] - 1 + 127, 0) - down, 1)
    scale = np.exp2(byte - 127.0)
    codes = (blocks / scale).astype(np.float32).astype(dtype).astype(np.float64)
    return np.moveaxis((codes * scale).reshape(v.shape), -1, axis)


WIDE = False


def mx_kscale(k):
    if not WIDE:
        return np.ones(k)
    levels = np.array([18, -18])
    if k % 512:
        return np.exp2(np.random.permutation(np.resize(levels, k // 32))).repeat(32)
    a = np.empty((k // 512, 16))
    for p in range(k // 512):
        a[p, :8] = np.random.permutation(np.resize(levels, 8))
        for g in range(8):
            far = levels[np.abs(levels - a[p, g]) >= 10]
            a[p, g + 8] = far[np.random.randint(len(far))]
    return np.exp2(a.ravel()).repeat(32)


def f64(x):
    return np.asarray(x).astype(np.float64)


def striped(idx):
    return np.tile(np.asarray(idx).reshape(-1, 16).T, (8, 1)).astype(np.uint16)


def unstriped(offs):
    return offs[:16].T.reshape(-1).astype(np.int64)

def planes(y):
    n, m = y.shape
    v = y.astype(np.float32).astype(ml_dtypes.bfloat16).astype(np.float64).reshape(n // 32, 32, m)
    top = np.abs(v).max(1)
    byte = np.clip(np.where(top > 0, np.frexp(top)[1] - 1 + 127 - 7, 1), 1, 254)
    codes = (v * np.exp2(127.0 - byte)[:, None, :]).reshape(n, m).astype(np.float32).astype(ml_dtypes.float8_e4m3fn).view(np.uint8)
    words = codes.reshape(n // 512, 128, 4, m).transpose(0, 1, 3, 2)
    return np.ascontiguousarray(words), np.ascontiguousarray(byte.astype(np.uint8).reshape(n // 512, 16, m))


N, T, D, V = 512, 2048, 512, 1024


def setup_inputs():
    n = np.random.standard_normal
    idx = np.random.permutation(T)[:N]
    s = mx_kscale(D)[:, None]
    z = mx_kscale(V)[:, None]
    w = n((D, V)) / np.sqrt(D)
    return {
        "xT": (n((D, T)) / s).astype(np.float32),
        "wd": (w * s).astype(np.float32),
        "wv": (w.T / z).astype(np.float32),
        "y": np.random.randint(0, 2, (V, N)).astype(np.float32),
        "cw": (np.random.uniform(0.5, 1.5, (V, 1)) / np.sqrt(V) * z).astype(np.float32),
        "rw": np.tile(np.random.uniform(0.5, 1.5, N), (128, 1)).astype(np.float32),
        "offs": striped(idx),
    }


def reference(xT, wd, wv, y, cw, rw, offs):
    idx = unstriped(offs)
    a = mxq(f64(wd), 0, "e4m3").T @ mxq(f64(xT)[:, idx], 0, "e4m3")
    g = f64(cw) * f64(rw)[:1] * (1.0 / (1.0 + np.exp(-a)) - f64(y))
    dx = mxq(f64(wv), 0, "e4m3").T @ mxq(g, 0, "e5m2")
    gx = np.zeros((D, T))
    gx[:, idx] = dx
    out_0 = gx
    return (out_0,) + planes(out_0)

@@ -1,0 +1,185 @@
+from contextlib import ExitStack
+
+import concourse.mybir as mybir
+
+N, T, D, V = 512, 2048, 512, 1024
+FLOPS = 2 * 2 * D * V * N
+
+F32 = mybir.dt.float32
+BF16 = mybir.dt.bfloat16
+I32 = mybir.dt.int32
+U32 = mybir.dt.uint32
+U16 = mybir.dt.uint16
+U8 = mybir.dt.uint8
+E4M3 = mybir.dt.float8_e4m3fn_x4
+E5M2 = mybir.dt.float8_e5m2_x4
+ACT = mybir.ActivationFunctionType
+ALU = mybir.AluOpType
+
+P = 128
+CHUNK = 512
+
+
+def tile_attend_gml_pl_nce_kernel(tc, xT, wd, wv, y, cw, rw, offs, out_0, out_1, out_2):
+    nc = tc.nc
+    with ExitStack() as ctx:
+        lists = ctx.enter_context(tc.tile_pool(name="lists", bufs=1))
+        sb = ctx.enter_context(tc.tile_pool(name="sb", bufs=1))
+        psum = ctx.enter_context(tc.psum_pool(name="psum", bufs=8))
+
+        def new(shape, dtype, name, tag=None):
+            return sb.tile(shape, dtype, name=name, tag=tag or name, align_bytes=64)
+
+        x_rows = xT.rearrange("(p t) c -> t p c", t=4)
+        x_win = [new([P, T], F32, "x_win%d" % t) for t in range(4)]
+        offsets = lists.tile([P, N // 16], U16, name="offsets")
+        cw_sb = new([P, 2, 4], F32, "cw_sb")
+        rw_sb = new([P, N], F32, "rw_sb")
+        wd_raw = [new([P, 4, 512], F32, "wd_raw%d" % g) for g in range(2)]
+        wv_raw = [new([P, 4, 512], F32, "wv_raw%d" % g) for g in range(2)]
+        y_sb = [new([P, 4, N], F32, "y_sb%d" % g) for g in range(2)]
+        wd_rows = wd.rearrange("(p j) v -> p j v", j=4)
+        wv_rows = wv.rearrange("(g p j) d -> g p j d", g=2, j=4)
+        y_rows = y.rearrange("(g p t) i -> g p t i", g=2, t=4)
+
+        nc.sync.dma_start(out=x_win[0][:], in_=x_rows[0])
+        nc.sync.dma_start(offsets[:], offs)
+        nc.scalar.dma_start(out=cw_sb[:], in_=cw.rearrange("(g p t) o -> p g (t o)", g=2, t=4))
+        nc.scalar.dma_start(out=rw_sb[:], in_=rw)
+        for t in range(1, 4):
+            nc.sync.dma_start(out=x_win[t][:], in_=x_rows[t])
+        for g in range(2):
+            nc.sync.dma_start(out=wd_raw[g][:], in_=wd_rows[:, :, 512 * g : 512 * (g + 1)])
+            nc.sync.dma_start(out=y_sb[g][:], in_=y_rows[g])
+        for g in range(2):
+            nc.sync.dma_start(out=wv_raw[g][:], in_=wv_rows[g])
+
+        warm = new([P, 8], F32, "warm")
+        nc.vector.memset(warm[:, 0:1], 0.0)
+        nc.scalar.activation(warm[:, 1:2], warm[:, 0:1], ACT.Sigmoid)
+        o_win = [new([P, T], F32, "o_win%d" % t) for t in range(4)]
+        for t in range(4):
+            nc.vector.memset(o_win[t][:], 0.0)
+        w_sb = [new([P, 4, N], F32, "w_sb%d" % g) for g in range(2)]
+        for g in range(2):
+            for t in range(4):
+                nc.scalar.activation(w_sb[g][:, t, :], rw_sb[:], ACT.Copy, scale=cw_sb[:, g, t : t + 1])
+
+        def quantize(grouped, width, fmt, name):
+            codes = new([P, width], U32, name + "_codes")
+            scales = new([P, width], U8, name + "_scales")
+            nc.vector.quantize_mx(out=codes[:].bitcast(fmt), scales=scales[:], in_=grouped)
+            return codes, scales
+
+        x_g = new([P, N, 4], BF16, "x_g")
+        for t in range(4):
+            nc.vector.tensor_copy(x_g[:, :, t], x_win[t][:].indirect(offsets[:]))
+        x_q = quantize(x_g[:].rearrange("p n t -> p (n t)"), N, E4M3, "x")
+
+        def deal(raw, h, name, on_vector):
+            dealt = new([P, 2, P, 4], BF16, name)
+            src = raw[:].rearrange("p j (m t) -> p m j t", t=4)[:, :, :, 2 * h : 2 * h + 2]
+            dst = dealt[:].rearrange("p t m j -> p m j t")
+            if on_vector:
+                nc.vector.tensor_copy(dst, src)
+            else:
+                nc.scalar.copy(dst, src)
+            return dealt
+
+        def quantize_half(dealt, name):
+            return quantize(dealt[:].rearrange("p t m j -> p (t m j)"), 2 * P, E4M3, name)
+
+        def stationary(halves, t):
+            codes, scales = halves[t // 2]
+            cols = slice(P * (t % 2), P * (t % 2 + 1))
+            return codes[:, cols].bitcast(E4M3), scales[:, cols]
+
+        s_sb = [new([P, 4, N], F32, "s_sb%d" % g) for g in range(2)]
+        g_g = [new([P, N, 4], BF16, "g_g%d" % g) for g in range(2)]
+
+        def scores(g, halves, ts):
+            for t in ts:
+                bank = psum.tile([P, N], F32, name="bank")
+                lhs, lhs_s = stationary(halves, t)
+                nc.tensor.matmul_mx(out=bank[:], lhsT=lhs, lhsT_scale=lhs_s, rhs=x_q[0][:].bitcast(E4M3), rhs_scale=x_q[1][:], start=True, stop=True)
+                nc.scalar.activation(s_sb[g][:, t, :], bank[:], ACT.Sigmoid)
+
+        def subtract(g):
+            for t in range(4):
+                nc.vector.tensor_tensor(s_sb[g][:, t, :], s_sb[g][:, t, :], y_sb[g][:, t, :], ALU.subtract)
+
+        def weigh(g, half):
+            cols = slice(256 * half, 256 * (half + 1))
+            nc.vector.tensor_tensor(
+                g_g[g][:, cols, :].rearrange("p (c i) t -> p c t i", i=4),
+                s_sb[g][:, :, cols].rearrange("p t (c i) -> p c t i", i=4),
+                w_sb[g][:, :, cols].rearrange("p t (c i) -> p c t i", i=4),
+                ALU.mult,
+            )
+
+        wd00 = deal(wd_raw[0], 0, "wd00", True)
+        wd01 = deal(wd_raw[0], 1, "wd01", False)
+        wd0_q = [quantize_half(wd00, "wd00"), quantize_half(wd01, "wd01")]
+        scores(0, wd0_q, range(4))
+        wd10 = deal(wd_raw[1], 0, "wd10", False)
+        wd11 = deal(wd_raw[1], 1, "wd11", False)
+        subtract(0)
+        weigh(0, 0)
+        wd1_q = [quantize_half(wd10, "wd10")]
+        weigh(0, 1)
+        wd1_q.append(quantize_half(wd11, "wd11"))
+        scores(1, wd1_q, range(4))
+        g_q = [quantize(g_g[0][:].rearrange("p n t -> p (n t)"), N, E5M2, "g0")]
+        wv_d = [[deal(wv_raw[g], h, "wv%d%d" % (g, h), False) for h in range(2)] for g in range(2)]
+        subtract(1)
+        weigh(1, 0)
+        wv_q = [[quantize_half(wv_d[0][h], "wv0%d" % h) for h in range(2)]]
+        weigh(1, 1)
+        wv_q.append([quantize_half(wv_d[1][0], "wv10")])
+        g_q.append(quantize(g_g[1][:].rearrange("p n t -> p (n t)"), N, E5M2, "g1"))
+        wv_q[1].append(quantize_half(wv_d[1][1], "wv11"))
+
+        banks = [psum.tile([P, N], F32, name="bank") for t in range(4)]
+        dx = [new([P, N], F32, "dx%d" % t) for t in range(4)]
+        for g in range(2):
+            for t in range(4):
+                lhs, lhs_s = stationary(wv_q[g], t)
+                nc.tensor.matmul_mx(out=banks[t][:], lhsT=lhs, lhsT_scale=lhs_s, rhs=g_q[g][0][:].bitcast(E5M2), rhs_scale=g_q[g][1][:], start=(g == 0), stop=(g == 1))
+        for t in range(4):
+            nc.scalar.copy(dx[t][:], banks[t][:])
+
+        out_rows = out_0.rearrange("(p t) c -> t p c", t=4)
+        chunks = T // CHUNK
+        pairs = [new([P, 2, CHUNK, 2], BF16, "pairs%d" % k, tag="y_sb%d" % k if k < 2 else "wd_raw%d" % (k - 2)) for k in range(chunks)]
+        for t in range(4):
+            nc.vector.tensor_copy(o_win[t][:].indirect(offsets[:]), dx[t][:])
+            nc.sync.dma_start(out=out_rows[t], in_=o_win[t][:])
+            for k in range(chunks):
+                nc.scalar.copy(pairs[k][:, t // 2, :, t % 2], o_win[t][:, CHUNK * k : CHUNK * (k + 1)])
+
+        words_out = out_1.rearrange("o p c l -> p (o c l)").bitcast(I32)
+        o_scales = new([P, T], U8, "o_scales")
+        woven = [new([P, CHUNK, 2, 2], BF16, "woven%d" % k, tag="x_win%d" % k) for k in range(chunks)]
+        o_codes = [new([P, CHUNK], U32, "o_codes%d" % k) for k in range(chunks)]
+
+        def weave(k):
+            src = pairs[k][:].rearrange("p u c e -> p c u e")
+            if k < chunks - 1:
+                nc.vector.tensor_copy(woven[k][:], src)
+            else:
+                nc.scalar.copy(woven[k][:], src)
+
+        def emit(k):
+            cols = slice(CHUNK * k, CHUNK * (k + 1))
+            nc.vector.quantize_mx(out=o_codes[k][:].bitcast(E4M3), scales=o_scales[:, cols], in_=woven[k][:].rearrange("p c u e -> p (c u e)"))
+            nc.sync.dma_start(out=words_out[:, cols], in_=o_codes[k][:].bitcast(I32))
+
+        weave(0)
+        for k in range(1, chunks):
+            weave(k)
+            emit(k - 1)
+        emit(chunks - 1)
+        scales_out = out_2.rearrange("o f c -> (o f) c").bitcast(I32)
+        for q in range(4):
+            queue = nc.scalar if q % 2 else nc.sync
+            queue.dma_start(out=scales_out[4 * q : 4 * q + 4, :], in_=o_scales[32 * q : 32 * q + 4, :].bitcast(I32))

@@ -1,6 +1,7 @@
 from contextlib import ExitStack
 
 import concourse.mybir as mybir
+from concourse.masks import make_identity
 
 N, T, D, V = 512, 2048, 512, 1024
 FLOPS = 2 * 2 * D * V * N
@@ -17,7 +18,8 @@ ACT = mybir.ActivationFunctionType
 ALU = mybir.AluOpType
 
 P = 128
-CHUNK = 512
+GROUPS = [(0, 1), (1, 3), (3, 5), (5, 7), (7, 8)]
+SPLIT = 6
 
 
 def tile_attend_gml_pl_nce_kernel(tc, xT, wd, wv, y, cw, rw, offs, out_0, out_1, out_2):
@@ -34,7 +36,7 @@ def tile_attend_gml_pl_nce_kernel(tc, xT, wd, wv, y, cw, rw, offs, out_0, out_1,
         x_win = [new([P, T], F32, "x_win%d" % t) for t in range(4)]
         offsets = lists.tile([P, N // 16], U16, name="offsets")
         cw_sb = new([P, 2, 4], F32, "cw_sb")
-        rw_sb = new([P, N], F32, "rw_sb")
+        rw_sb = new([P, 4], F32, "rw_sb")
         wd_raw = [new([P, 4, 512], F32, "wd_raw%d" % g) for g in range(2)]
         wv_raw = [new([P, 4, 512], F32, "wv_raw%d" % g) for g in range(2)]
         y_sb = [new([P, 4, N], F32, "y_sb%d" % g) for g in range(2)]
@@ -45,7 +47,7 @@ def tile_attend_gml_pl_nce_kernel(tc, xT, wd, wv, y, cw, rw, offs, out_0, out_1,
         nc.sync.dma_start(out=x_win[0][:], in_=x_rows[0])
         nc.sync.dma_start(offsets[:], offs)
         nc.scalar.dma_start(out=cw_sb[:], in_=cw.rearrange("(g p t) o -> p g (t o)", g=2, t=4))
-        nc.scalar.dma_start(out=rw_sb[:], in_=rw)
+        nc.scalar.dma_start(out=rw_sb[:], in_=rw[0:1, :].rearrange("o (p c) -> (o p) c", c=4))
         for t in range(1, 4):
             nc.sync.dma_start(out=x_win[t][:], in_=x_rows[t])
         for g in range(2):
@@ -60,13 +62,20 @@ def tile_attend_gml_pl_nce_kernel(tc, xT, wd, wv, y, cw, rw, offs, out_0, out_1,
         o_win = [new([P, T], F32, "o_win%d" % t) for t in range(4)]
         for t in range(4):
             nc.vector.memset(o_win[t][:], 0.0)
-        w_sb = [new([P, 4, N], F32, "w_sb%d" % g) for g in range(2)]
+        ident = new([P, P], F32, "ident")
+        make_identity(nc, ident[:])
+        rw_bank = psum.tile([P, 4, P], F32, name="bank")
+        for c in range(4):
+            nc.tensor.transpose(rw_bank[:, c, :], rw_sb[:, c : c + 1].to_broadcast([P, P]), ident[:])
+        rw_all = rw_bank[:].rearrange("p c n -> p n c")
+        w_sb = [[new([P, 4, N // 2], F32, "w_sb%d%d" % (g, h)) for h in range(2)] for g in range(2)]
         for g in range(2):
-            for t in range(4):
-                nc.scalar.activation(w_sb[g][:, t, :], rw_sb[:], ACT.Copy, scale=cw_sb[:, g, t : t + 1])
+            for h in range(2):
+                for t in range(4):
+                    nc.scalar.activation(w_sb[g][h][:, t, :].rearrange("p (n c) -> p n c", c=4), rw_all[:, 64 * h : 64 * (h + 1), :], ACT.Copy, scale=cw_sb[:, g, t : t + 1])
 
-        def quantize(grouped, width, fmt, name):
-            codes = new([P, width], U32, name + "_codes")
+        def quantize(grouped, width, fmt, name, tag=None):
+            codes = new([P, width], U32, name + "_codes", tag)
             scales = new([P, width], U8, name + "_scales")
             nc.vector.quantize_mx(out=codes[:].bitcast(fmt), scales=scales[:], in_=grouped)
             return codes, scales
@@ -76,8 +85,8 @@ def tile_attend_gml_pl_nce_kernel(tc, xT, wd, wv, y, cw, rw, offs, out_0, out_1,
             nc.vector.tensor_copy(x_g[:, :, t], x_win[t][:].indirect(offsets[:]))
         x_q = quantize(x_g[:].rearrange("p n t -> p (n t)"), N, E4M3, "x")
 
-        def deal(raw, h, name, on_vector):
-            dealt = new([P, 2, P, 4], BF16, name)
+        def deal(raw, h, name, on_vector, tag=None):
+            dealt = new([P, 2, P, 4], BF16, name, tag)
             src = raw[:].rearrange("p j (m t) -> p m j t", t=4)[:, :, :, 2 * h : 2 * h + 2]
             dst = dealt[:].rearrange("p t m j -> p m j t")
             if on_vector:
@@ -86,34 +95,36 @@ def tile_attend_gml_pl_nce_kernel(tc, xT, wd, wv, y, cw, rw, offs, out_0, out_1,
                 nc.scalar.copy(dst, src)
             return dealt
 
-        def quantize_half(dealt, name):
-            return quantize(dealt[:].rearrange("p t m j -> p (t m j)"), 2 * P, E4M3, name)
+        def quantize_half(dealt, name, tag=None):
+            return quantize(dealt[:].rearrange("p t m j -> p (t m j)"), 2 * P, E4M3, name, tag)
 
         def stationary(halves, t):
             codes, scales = halves[t // 2]
             cols = slice(P * (t % 2), P * (t % 2 + 1))
             return codes[:, cols].bitcast(E4M3), scales[:, cols]
 
-        s_sb = [new([P, 4, N], F32, "s_sb%d" % g) for g in range(2)]
-        g_g = [new([P, N, 4], BF16, "g_g%d" % g) for g in range(2)]
+        s_sb = [[new([P, N], F32, "s_sb%d%d" % (g, t)) for t in range(4)] for g in range(2)]
+        g_g = {}
 
         def scores(g, halves, ts):
             for t in ts:
                 bank = psum.tile([P, N], F32, name="bank")
                 lhs, lhs_s = stationary(halves, t)
                 nc.tensor.matmul_mx(out=bank[:], lhsT=lhs, lhsT_scale=lhs_s, rhs=x_q[0][:].bitcast(E4M3), rhs_scale=x_q[1][:], start=True, stop=True)
-                nc.scalar.activation(s_sb[g][:, t, :], bank[:], ACT.Sigmoid)
+                nc.scalar.activation(s_sb[g][t][:], bank[:], ACT.Sigmoid)
 
         def subtract(g):
             for t in range(4):
-                nc.vector.tensor_tensor(s_sb[g][:, t, :], s_sb[g][:, t, :], y_sb[g][:, t, :], ALU.subtract)
+                for cols in [slice(0, N)] if t < 3 else [slice(0, 256), slice(256, N)]:
+                    nc.vector.tensor_tensor(y_sb[g][:, t, cols], s_sb[g][t][:, cols], y_sb[g][:, t, cols], ALU.subtract)
 
-        def weigh(g, half):
+        def weigh(g, half, tag=None):
             cols = slice(256 * half, 256 * (half + 1))
+            g_g[g, half] = new([P, N // 2, 4], BF16, "g_g%d%d" % (g, half), tag)
             nc.vector.tensor_tensor(
-                g_g[g][:, cols, :].rearrange("p (c i) t -> p c t i", i=4),
-                s_sb[g][:, :, cols].rearrange("p t (c i) -> p c t i", i=4),
-                w_sb[g][:, :, cols].rearrange("p t (c i) -> p c t i", i=4),
+                g_g[g, half][:].rearrange("p (c i) t -> p c t i", i=4),
+                y_sb[g][:, :, cols].rearrange("p t (c i) -> p c t i", i=4),
+                w_sb[g][half][:].rearrange("p t (c i) -> p c t i", i=4),
                 ALU.mult,
             )
 
@@ -123,55 +134,86 @@ def tile_attend_gml_pl_nce_kernel(tc, xT, wd, wv, y, cw, rw, offs, out_0, out_1,
         scores(0, wd0_q, range(4))
         wd10 = deal(wd_raw[1], 0, "wd10", False)
         wd11 = deal(wd_raw[1], 1, "wd11", False)
+        g_q = {}
+
+        def quantize_g(g, half, tag=None):
+            if g not in g_q:
+                g_q[g] = (new([P, N], U32, "g%d_codes" % g, tag), new([P, N], U8, "g%d_scales" % g))
+            cols = slice(256 * half, 256 * (half + 1))
+            nc.vector.quantize_mx(out=g_q[g][0][:, cols].bitcast(E5M2), scales=g_q[g][1][:, cols], in_=g_g[g, half][:].rearrange("p n t -> p (n t)"))
+
         subtract(0)
         weigh(0, 0)
-        wd1_q = [quantize_half(wd10, "wd10")]
-        weigh(0, 1)
-        wd1_q.append(quantize_half(wd11, "wd11"))
+        wd1_q = [quantize_half(wd10, "wd10", "s_sb03")]
+        wd1_q.append(quantize_half(wd11, "wd11", "w_sb00"))
+        quantize_g(0, 0, "wd10")
+        weigh(0, 1, "wd11")
         scores(1, wd1_q, range(4))
-        g_q = [quantize(g_g[0][:].rearrange("p n t -> p (n t)"), N, E5M2, "g0")]
-        wv_d = [[deal(wv_raw[g], h, "wv%d%d" % (g, h), False) for h in range(2)] for g in range(2)]
-        subtract(1)
-        weigh(1, 0)
-        wv_q = [[quantize_half(wv_d[0][h], "wv0%d" % h) for h in range(2)]]
-        weigh(1, 1)
-        wv_q.append([quantize_half(wv_d[1][0], "wv10")])
-        g_q.append(quantize(g_g[1][:].rearrange("p n t -> p (n t)"), N, E5M2, "g1"))
-        wv_q[1].append(quantize_half(wv_d[1][1], "wv11"))
+        def deal_wv(h, tag):
+            dealt = new([P, 2, 2, P, 4], BF16, "wv_dealt%d" % h, tag)
+            for g in range(2):
+                src = wv_raw[g][:].rearrange("p j (m t) -> p m j t", t=4)[:, :, :, 2 * h : 2 * h + 2]
+                nc.scalar.copy(dealt[:, g].rearrange("p t m j -> p m j t"), src)
+            return dealt[:].rearrange("p g t m j -> p (g t m j)")
 
-        banks = [psum.tile([P, N], F32, name="bank") for t in range(4)]
-        dx = [new([P, N], F32, "dx%d" % t) for t in range(4)]
-        for g in range(2):
-            for t in range(4):
-                lhs, lhs_s = stationary(wv_q[g], t)
-                nc.tensor.matmul_mx(out=banks[t][:], lhsT=lhs, lhsT_scale=lhs_s, rhs=g_q[g][0][:].bitcast(E5M2), rhs_scale=g_q[g][1][:], start=(g == 0), stop=(g == 1))
-        for t in range(4):
-            nc.scalar.copy(dx[t][:], banks[t][:])
+        wv00 = deal(wv_raw[0], 0, "wv00", False, "x_codes")
+        wv10 = deal(wv_raw[1], 0, "wv10", False, "x_scales")
+        subtract(1)
+        quantize_g(0, 1)
+        g_g1 = new([P, N, 4], BF16, "g_g1")
+        for half in range(2):
+            cols = slice(256 * half, 256 * (half + 1))
+            nc.vector.tensor_tensor(
+                g_g1[:, cols, :].rearrange("p (c i) t -> p c t i", i=4),
+                y_sb[1][:, :, cols].rearrange("p t (c i) -> p c t i", i=4),
+                w_sb[1][half][:].rearrange("p t (c i) -> p c t i", i=4),
+                ALU.mult,
+            )
+        wv_a = [quantize_half(wv00, "wv00", "s_sb13"), quantize_half(wv10, "wv10", "w_sb10")]
+        g_q[1] = quantize(g_g1[:].rearrange("p n t -> p (n t)"), N, E5M2, "g1", "x_scales")
+        wv_b = quantize(deal_wv(1, "wd11_scales"), 4 * P, E4M3, "wv_b", "g_g1")
+
+        dx_pair = [new([P, 2, N], F32, "dx%d" % h, None if h else "wd11_scales") for h in range(2)]
+        dx = [dx_pair[t // 2][:, t % 2, :] for t in range(4)]
+        for h in range(2):
+            banks = [psum.tile([P, N], F32, name="bank") for t in range(2)]
+            for g in range(2):
+                for t in (2 * h, 2 * h + 1):
+                    first = P * (t % 2) + 2 * P * g * h
+                    codes, scales = wv_b if h else wv_a[g]
+                    lhs, lhs_s = codes[:, first : first + P].bitcast(E4M3), scales[:, first : first + P]
+                    nc.tensor.matmul_mx(out=banks[t % 2][:], lhsT=lhs, lhsT_scale=lhs_s, rhs=g_q[g][0][:].bitcast(E5M2), rhs_scale=g_q[g][1][:], start=(g == 0), stop=(g == 1))
+            for t in (2 * h, 2 * h + 1):
+                nc.scalar.copy(dx[t], banks[t % 2][:])
 
         out_rows = out_0.rearrange("(p t) c -> t p c", t=4)
-        chunks = T // CHUNK
-        pairs = [new([P, 2, CHUNK, 2], BF16, "pairs%d" % k, tag="y_sb%d" % k if k < 2 else "wd_raw%d" % (k - 2)) for k in range(chunks)]
+        pairs = new([P, 8, 2, 256, 2], BF16, "pairs", "g_g1")
         for t in range(4):
-            nc.vector.tensor_copy(o_win[t][:].indirect(offsets[:]), dx[t][:])
+            nc.vector.tensor_copy(o_win[t][:].indirect(offsets[:]), dx[t])
             nc.sync.dma_start(out=out_rows[t], in_=o_win[t][:])
-            for k in range(chunks):
-                nc.scalar.copy(pairs[k][:, t // 2, :, t % 2], o_win[t][:, CHUNK * k : CHUNK * (k + 1)])
+            for lo, hi in [(0, 8)] if t < 3 else GROUPS:
+                nc.scalar.copy(pairs[:, lo:hi, t // 2, :, t % 2], o_win[t][:, 256 * lo : 256 * hi].rearrange("p (k c) -> p k c", c=256))
 
         words_out = out_1.rearrange("o p c l -> p (o c l)").bitcast(I32)
         o_scales = new([P, T], U8, "o_scales")
-        woven = [new([P, CHUNK, 2, 2], BF16, "woven%d" % k, tag="x_win%d" % k) for k in range(chunks)]
-        o_codes = [new([P, CHUNK], U32, "o_codes%d" % k) for k in range(chunks)]
+        chunks = len(GROUPS)
+        reuse = ["x_win0", "x_win1", "x_win2", "x_win3", "s_sb00"]
+        woven = [new([P, hi - lo, 256, 2, 2], BF16, "woven%d" % k, tag=reuse[k]) for k, (lo, hi) in enumerate(GROUPS)]
+        o_codes = [new([P, 256 * (hi - lo)], U32, "o_codes%d" % k) for k, (lo, hi) in enumerate(GROUPS)]
 
         def weave(k):
-            src = pairs[k][:].rearrange("p u c e -> p c u e")
-            if k < chunks - 1:
-                nc.vector.tensor_copy(woven[k][:], src)
-            else:
-                nc.scalar.copy(woven[k][:], src)
+            lo, hi = GROUPS[k]
+            mid = min(max(lo, SPLIT), hi)
+            dst = woven[k][:].rearrange("p k c u e -> p k c (u e)")
+            src = pairs[:].rearrange("p k u c e -> p k u (c e)")
+            if mid > lo:
+                nc.vector.tensor_copy(dst[:, : mid - lo].bitcast(I32), src[:, lo:mid].bitcast(I32).rearrange("p k u c -> p k c u"))
+            if hi > mid:
+                nc.scalar.copy(dst[:, mid - lo :].bitcast(U32), src[:, mid:hi].bitcast(U32).rearrange("p k u c -> p k c u"))
 
         def emit(k):
-            cols = slice(CHUNK * k, CHUNK * (k + 1))
-            nc.vector.quantize_mx(out=o_codes[k][:].bitcast(E4M3), scales=o_scales[:, cols], in_=woven[k][:].rearrange("p c u e -> p (c u e)"))
+            cols = slice(256 * GROUPS[k][0], 256 * GROUPS[k][1])
+            nc.vector.quantize_mx(out=o_codes[k][:].bitcast(E4M3), scales=o_scales[:, cols], in_=woven[k][:].rearrange("p k c u e -> p (k c u e)"))
             nc.sync.dma_start(out=words_out[:, cols], in_=o_codes[k][:].bitcast(I32))
 
         weave(0)

@@ -52,7 +52,9 @@ def tile_attend_gml_pl_nce_kernel(tc, xT, wd, wv, y, cw, rw, offs, out_0, out_1,
             nc.sync.dma_start(out=x_win[t][:], in_=x_rows[t])
         for g in range(2):
             nc.sync.dma_start(out=wd_raw[g][:], in_=wd_rows[:, :, 512 * g : 512 * (g + 1)])
-            nc.sync.dma_start(out=y_sb[g][:], in_=y_rows[g])
+        for lanes in (slice(0, 1), slice(1, 2), slice(2, 4)):
+            nc.sync.dma_start(out=y_sb[0][:, lanes, :], in_=y_rows[0][:, lanes, :])
+        nc.sync.dma_start(out=y_sb[1][:], in_=y_rows[1])
         for g in range(2):
             nc.sync.dma_start(out=wv_raw[g][:], in_=wv_rows[g])
 
@@ -68,11 +70,11 @@ def tile_attend_gml_pl_nce_kernel(tc, xT, wd, wv, y, cw, rw, offs, out_0, out_1,
         for c in range(4):
             nc.tensor.transpose(rw_bank[:, c, :], rw_sb[:, c : c + 1].to_broadcast([P, P]), ident[:])
         rw_all = rw_bank[:].rearrange("p c n -> p n c")
-        w_sb = [[new([P, 4, N // 2], F32, "w_sb%d%d" % (g, h)) for h in range(2)] for g in range(2)]
-        for g in range(2):
-            for h in range(2):
-                for t in range(4):
-                    nc.scalar.activation(w_sb[g][h][:, t, :].rearrange("p (n c) -> p n c", c=4), rw_all[:, 64 * h : 64 * (h + 1), :], ACT.Copy, scale=cw_sb[:, g, t : t + 1])
+        w_cols = [(0, slice(0, 64)), (0, slice(64, 128)), (1, slice(0, 128))]
+        w_sb = [new([P, quads.stop - quads.start, 4, 4], F32, "w_sb%d" % k) for k, (g, quads) in enumerate(w_cols)]
+        for k, (g, quads) in enumerate(w_cols):
+            for t in range(4):
+                nc.scalar.activation(w_sb[k][:, :, t, :], rw_all[:, quads, :], ACT.Copy, scale=cw_sb[:, g, t : t + 1])
 
         def quantize(grouped, width, fmt, name, tag=None):
             codes = new([P, width], U32, name + "_codes", tag)
@@ -103,52 +105,51 @@ def tile_attend_gml_pl_nce_kernel(tc, xT, wd, wv, y, cw, rw, offs, out_0, out_1,
             cols = slice(P * (t % 2), P * (t % 2 + 1))
             return codes[:, cols].bitcast(E4M3), scales[:, cols]
 
-        s_sb = [[new([P, N], F32, "s_sb%d%d" % (g, t)) for t in range(4)] for g in range(2)]
-        g_g = {}
+        s_lanes = [[slice(t, t + 1) for t in range(4)], [slice(0, 2), slice(2, 4)]]
+        s_sb = [[new([P, lanes.stop - lanes.start, N], F32, "s_sb%d%d" % (g, lanes.start)) for lanes in s_lanes[g]] for g in range(2)]
+        halves = [slice(0, N // 2), slice(N // 2, N)]
 
-        def scores(g, halves, ts):
-            for t in ts:
-                bank = psum.tile([P, N], F32, name="bank")
-                lhs, lhs_s = stationary(halves, t)
-                nc.tensor.matmul_mx(out=bank[:], lhsT=lhs, lhsT_scale=lhs_s, rhs=x_q[0][:].bitcast(E4M3), rhs_scale=x_q[1][:], start=True, stop=True)
-                nc.scalar.activation(s_sb[g][t][:], bank[:], ACT.Sigmoid)
+        def scores(g, wd_q):
+            for k, lanes in enumerate(s_lanes[g]):
+                for t in range(lanes.start, lanes.stop):
+                    bank = psum.tile([P, N], F32, name="bank")
+                    lhs, lhs_s = stationary(wd_q, t)
+                    nc.tensor.matmul_mx(out=bank[:], lhsT=lhs, lhsT_scale=lhs_s, rhs=x_q[0][:].bitcast(E4M3), rhs_scale=x_q[1][:], start=True, stop=True)
+                    for cols in halves if (g, t) == (0, 3) else [slice(0, N)]:
+                        nc.scalar.activation(s_sb[g][k][:, t - lanes.start, cols], bank[:, cols], ACT.Sigmoid)
 
         def subtract(g):
-            for t in range(4):
-                for cols in [slice(0, N)] if t < 3 else [slice(0, 256), slice(256, N)]:
-                    nc.vector.tensor_tensor(y_sb[g][:, t, cols], s_sb[g][t][:, cols], y_sb[g][:, t, cols], ALU.subtract)
+            for k, lanes in enumerate(s_lanes[g]):
+                for cols in halves if (g, k) == (0, 3) else [slice(0, N)]:
+                    nc.vector.tensor_tensor(y_sb[g][:, lanes, cols], s_sb[g][k][:, :, cols], y_sb[g][:, lanes, cols], ALU.subtract)
 
-        def weigh(g, half, tag=None):
-            cols = slice(256 * half, 256 * (half + 1))
-            g_g[g, half] = new([P, N // 2, 4], BF16, "g_g%d%d" % (g, half), tag)
+        def weigh(k, tag=None):
+            g, quads = w_cols[k]
+            width = 4 * (quads.stop - quads.start)
+            grad = new([P, width, 4], BF16, "grad%d" % k, tag)
             nc.vector.tensor_tensor(
-                g_g[g, half][:].rearrange("p (c i) t -> p c t i", i=4),
-                y_sb[g][:, :, cols].rearrange("p t (c i) -> p c t i", i=4),
-                w_sb[g][half][:].rearrange("p t (c i) -> p c t i", i=4),
+                grad[:].rearrange("p (c i) t -> p c t i", i=4),
+                y_sb[g][:].rearrange("p t (c i) -> p c t i", i=4)[:, quads],
+                w_sb[k][:],
                 ALU.mult,
             )
+            return grad[:].rearrange("p n t -> p (n t)")
 
         wd00 = deal(wd_raw[0], 0, "wd00", True)
         wd01 = deal(wd_raw[0], 1, "wd01", False)
         wd0_q = [quantize_half(wd00, "wd00"), quantize_half(wd01, "wd01")]
-        scores(0, wd0_q, range(4))
-        wd10 = deal(wd_raw[1], 0, "wd10", False)
-        wd11 = deal(wd_raw[1], 1, "wd11", False)
-        g_q = {}
-
-        def quantize_g(g, half, tag=None):
-            if g not in g_q:
-                g_q[g] = (new([P, N], U32, "g%d_codes" % g, tag), new([P, N], U8, "g%d_scales" % g))
-            cols = slice(256 * half, 256 * (half + 1))
-            nc.vector.quantize_mx(out=g_q[g][0][:, cols].bitcast(E5M2), scales=g_q[g][1][:, cols], in_=g_g[g, half][:].rearrange("p n t -> p (n t)"))
-
+        scores(0, wd0_q)
+        wd10 = deal(wd_raw[1], 0, "wd10", True)
+        wd1_q = [quantize_half(wd10, "wd10")]
+        wd11 = deal(wd_raw[1], 1, "wd11", False, "wd01_codes")
         subtract(0)
-        weigh(0, 0)
-        wd1_q = [quantize_half(wd10, "wd10", "s_sb03")]
-        wd1_q.append(quantize_half(wd11, "wd11", "w_sb00"))
-        quantize_g(0, 0, "wd10")
-        weigh(0, 1, "wd11")
-        scores(1, wd1_q, range(4))
+        grad0a = weigh(0)
+        wd1_q.append(quantize_half(wd11, "wd11", "s_sb03"))
+        g0_codes, g0_scales = new([P, N], U32, "g0_codes"), new([P, N], U8, "g0_scales")
+        nc.vector.quantize_mx(out=g0_codes[:, halves[0]].bitcast(E5M2), scales=g0_scales[:, halves[0]], in_=grad0a)
+        grad0b = weigh(1, "wd01_codes")
+        scores(1, wd1_q)
+
         def deal_wv(h, tag):
             dealt = new([P, 2, 2, P, 4], BF16, "wv_dealt%d" % h, tag)
             for g in range(2):
@@ -159,19 +160,12 @@ def tile_attend_gml_pl_nce_kernel(tc, xT, wd, wv, y, cw, rw, offs, out_0, out_1,
         wv00 = deal(wv_raw[0], 0, "wv00", False, "x_codes")
         wv10 = deal(wv_raw[1], 0, "wv10", False, "x_scales")
         subtract(1)
-        quantize_g(0, 1)
-        g_g1 = new([P, N, 4], BF16, "g_g1")
-        for half in range(2):
-            cols = slice(256 * half, 256 * (half + 1))
-            nc.vector.tensor_tensor(
-                g_g1[:, cols, :].rearrange("p (c i) t -> p c t i", i=4),
-                y_sb[1][:, :, cols].rearrange("p t (c i) -> p c t i", i=4),
-                w_sb[1][half][:].rearrange("p t (c i) -> p c t i", i=4),
-                ALU.mult,
-            )
-        wv_a = [quantize_half(wv00, "wv00", "s_sb13"), quantize_half(wv10, "wv10", "w_sb10")]
-        g_q[1] = quantize(g_g1[:].rearrange("p n t -> p (n t)"), N, E5M2, "g1", "x_scales")
-        wv_b = quantize(deal_wv(1, "wd11_scales"), 4 * P, E4M3, "wv_b", "g_g1")
+        nc.vector.quantize_mx(out=g0_codes[:, halves[1]].bitcast(E5M2), scales=g0_scales[:, halves[1]], in_=grad0b)
+        wv_a = [quantize_half(wv00, "wv00", "s_sb10")]
+        grad1 = weigh(2)
+        wv_a.append(quantize_half(wv10, "wv10", "s_sb12"))
+        g_q = [(g0_codes, g0_scales), quantize(grad1, N, E5M2, "g1", "x_scales")]
+        wv_b = quantize(deal_wv(1, "wd11_scales"), 4 * P, E4M3, "wv_b", "grad2")
 
         dx_pair = [new([P, 2, N], F32, "dx%d" % h, None if h else "wd11_scales") for h in range(2)]
         dx = [dx_pair[t // 2][:, t % 2, :] for t in range(4)]
@@ -187,7 +181,7 @@ def tile_attend_gml_pl_nce_kernel(tc, xT, wd, wv, y, cw, rw, offs, out_0, out_1,
                 nc.scalar.copy(dx[t], banks[t % 2][:])
 
         out_rows = out_0.rearrange("(p t) c -> t p c", t=4)
-        pairs = new([P, 8, 2, 256, 2], BF16, "pairs", "g_g1")
+        pairs = new([P, 8, 2, 256, 2], BF16, "pairs", "grad2")
         for t in range(4):
             nc.vector.tensor_copy(o_win[t][:].indirect(offsets[:]), dx[t])
             nc.sync.dma_start(out=out_rows[t], in_=o_win[t][:])

@@ -62,10 +62,12 @@ def tile_attend_gml_pl_nce_kernel(tc, xT, wd, wv, y, cw, rw, offs, out_0, out_1,
         nc.vector.memset(warm[:, 0:1], 0.0)
         nc.scalar.activation(warm[:, 1:2], warm[:, 0:1], ACT.Sigmoid)
         o_win = [new([P, T], F32, "o_win%d" % t) for t in range(4)]
-        for t in range(4):
-            nc.vector.memset(o_win[t][:], 0.0)
+        for t in range(2):
+            nc.vector.memset(o_win[t][:].bitcast(I32), 0)
         ident = new([P, P], F32, "ident")
         make_identity(nc, ident[:])
+        for t in range(2, 4):
+            nc.gpsimd.memset(o_win[t][:].bitcast(I32), 0)
         rw_bank = psum.tile([P, 4, P], F32, name="bank")
         for c in range(4):
             nc.tensor.transpose(rw_bank[:, c, :], rw_sb[:, c : c + 1].to_broadcast([P, P]), ident[:])
@@ -118,8 +120,9 @@ def tile_attend_gml_pl_nce_kernel(tc, xT, wd, wv, y, cw, rw, offs, out_0, out_1,
                     for cols in halves if (g, t) == (0, 3) else [slice(0, N)]:
                         nc.scalar.activation(s_sb[g][k][:, t - lanes.start, cols], bank[:, cols], ACT.Sigmoid)
 
-        def subtract(g):
-            for k, lanes in enumerate(s_lanes[g]):
+        def subtract(g, ks):
+            for k in ks:
+                lanes = s_lanes[g][k]
                 for cols in halves if (g, k) == (0, 3) else [slice(0, N)]:
                     nc.vector.tensor_tensor(y_sb[g][:, lanes, cols], s_sb[g][k][:, :, cols], y_sb[g][:, lanes, cols], ALU.subtract)
 
@@ -140,9 +143,10 @@ def tile_attend_gml_pl_nce_kernel(tc, xT, wd, wv, y, cw, rw, offs, out_0, out_1,
         wd0_q = [quantize_half(wd00, "wd00"), quantize_half(wd01, "wd01")]
         scores(0, wd0_q)
         wd10 = deal(wd_raw[1], 0, "wd10", True)
+        subtract(0, [0])
         wd1_q = [quantize_half(wd10, "wd10")]
         wd11 = deal(wd_raw[1], 1, "wd11", False, "wd01_codes")
-        subtract(0)
+        subtract(0, [1, 2, 3])
         grad0a = weigh(0)
         wd1_q.append(quantize_half(wd11, "wd11", "s_sb03"))
         g0_codes, g0_scales = new([P, N], U32, "g0_codes"), new([P, N], U8, "g0_scales")
@@ -159,7 +163,7 @@ def tile_attend_gml_pl_nce_kernel(tc, xT, wd, wv, y, cw, rw, offs, out_0, out_1,
 
         wv00 = deal(wv_raw[0], 0, "wv00", False, "x_codes")
         wv10 = deal(wv_raw[1], 0, "wv10", False, "x_scales")
-        subtract(1)
+        subtract(1, [0, 1])
         nc.vector.quantize_mx(out=g0_codes[:, halves[1]].bitcast(E5M2), scales=g0_scales[:, halves[1]], in_=grad0b)
         wv_a = [quantize_half(wv00, "wv00", "s_sb10")]
         grad1 = weigh(2)

@@ -18,8 +18,8 @@ ACT = mybir.ActivationFunctionType
 ALU = mybir.AluOpType
 
 P = 128
-GROUPS = [(0, 1), (1, 3), (3, 5), (5, 7), (7, 8)]
-SPLIT = 6
+GROUPS = [(7, 8), (0, 2), (2, 4), (4, 6), (6, 7)]
+SPLIT = 5
 
 
 def tile_attend_gml_pl_nce_kernel(tc, xT, wd, wv, y, cw, rw, offs, out_0, out_1, out_2):
@@ -162,17 +162,19 @@ def tile_attend_gml_pl_nce_kernel(tc, xT, wd, wv, y, cw, rw, offs, out_0, out_1,
             return dealt[:].rearrange("p g t m j -> p (g t m j)")
 
         wv00 = deal(wv_raw[0], 0, "wv00", False, "x_codes")
-        wv10 = deal(wv_raw[1], 0, "wv10", False, "x_scales")
+        wv10 = deal(wv_raw[1], 0, "wv10", False)
         subtract(1, [0, 1])
         nc.vector.quantize_mx(out=g0_codes[:, halves[1]].bitcast(E5M2), scales=g0_scales[:, halves[1]], in_=grad0b)
-        wv_a = [quantize_half(wv00, "wv00", "s_sb10")]
         grad1 = weigh(2)
-        wv_a.append(quantize_half(wv10, "wv10", "s_sb12"))
-        g_q = [(g0_codes, g0_scales), quantize(grad1, N, E5M2, "g1", "x_scales")]
-        wv_b = quantize(deal_wv(1, "wd11_scales"), 4 * P, E4M3, "wv_b", "grad2")
+        wv_a = [quantize_half(wv00, "wv00", "wd01_codes")]
+        g_q = [(g0_codes, g0_scales), quantize(grad1, N, E5M2, "g1")]
+        wv_a.append(quantize_half(wv10, "wv10", "w_sb2"))
+        wv_b = quantize(deal_wv(1, "wd11_scales"), 4 * P, E4M3, "wv_b", "x_codes")
 
-        dx_pair = [new([P, 2, N], F32, "dx%d" % h, None if h else "wd11_scales") for h in range(2)]
-        dx = [dx_pair[t // 2][:, t % 2, :] for t in range(4)]
+        dx_pair = new([P, 2, N], F32, "dx0", "wd11_scales")
+        dx_third = new([P, N], F32, "dx2")
+        stage = new([P, 2 * T + 256], F32, "stage", "x_codes")
+        dx = [dx_pair[:, 0, :], dx_pair[:, 1, :], dx_third[:], stage[:, 2 * T - 256 :]]
         for h in range(2):
             banks = [psum.tile([P, N], F32, name="bank") for t in range(2)]
             for g in range(2):
@@ -185,12 +187,15 @@ def tile_attend_gml_pl_nce_kernel(tc, xT, wd, wv, y, cw, rw, offs, out_0, out_1,
                 nc.scalar.copy(dx[t], banks[t % 2][:])
 
         out_rows = out_0.rearrange("(p t) c -> t p c", t=4)
-        pairs = new([P, 8, 2, 256, 2], BF16, "pairs", "grad2")
+        pairs = stage[:, : 2 * T].bitcast(BF16).rearrange("p (k u c e) -> p k u c e", k=8, u=2, e=2)
         for t in range(4):
             nc.vector.tensor_copy(o_win[t][:].indirect(offsets[:]), dx[t])
             nc.sync.dma_start(out=out_rows[t], in_=o_win[t][:])
-            for lo, hi in [(0, 8)] if t < 3 else GROUPS:
+            for lo, hi in [[(0, 8)], [(0, 8)], [(0, 7)], GROUPS[1:]][t]:
                 nc.scalar.copy(pairs[:, lo:hi, t // 2, :, t % 2], o_win[t][:, 256 * lo : 256 * hi].rearrange("p (k c) -> p k c", c=256))
+
+        for t in (3, 2):
+            nc.vector.tensor_copy(pairs[:, 7, 1, :, t % 2], o_win[t][:, T - 256 :])
 
         words_out = out_1.rearrange("o p c l -> p (o c l)").bitcast(I32)
         o_scales = new([P, T], U8, "o_scales")
@@ -201,9 +206,9 @@ def tile_attend_gml_pl_nce_kernel(tc, xT, wd, wv, y, cw, rw, offs, out_0, out_1,
 
         def weave(k):
             lo, hi = GROUPS[k]
-            mid = min(max(lo, SPLIT), hi)
+            mid = min(max(lo, SPLIT), hi) if k else hi
             dst = woven[k][:].rearrange("p k c u e -> p k c (u e)")
-            src = pairs[:].rearrange("p k u c e -> p k u (c e)")
+            src = pairs.rearrange("p k u c e -> p k u (c e)")
             if mid > lo:
                 nc.vector.tensor_copy(dst[:, : mid - lo].bitcast(I32), src[:, lo:mid].bitcast(I32).rearrange("p k u c -> p k c u"))
             if hi > mid:

@@ -52,7 +52,7 @@ def tile_attend_gml_pl_nce_kernel(tc, xT, wd, wv, y, cw, rw, offs, out_0, out_1,
             nc.sync.dma_start(out=x_win[t][:], in_=x_rows[t])
         for g in range(2):
             nc.sync.dma_start(out=wd_raw[g][:], in_=wd_rows[:, :, 512 * g : 512 * (g + 1)])
-        for lanes in (slice(0, 1), slice(1, 2), slice(2, 4)):
+        for lanes in (slice(t, t + 1) for t in range(4)):
             nc.sync.dma_start(out=y_sb[0][:, lanes, :], in_=y_rows[0][:, lanes, :])
         nc.sync.dma_start(out=y_sb[1][:], in_=y_rows[1])
         for g in range(2):
@@ -168,10 +168,14 @@ def tile_attend_gml_pl_nce_kernel(tc, xT, wd, wv, y, cw, rw, offs, out_0, out_1,
         grad1 = weigh(2)
         wv_a = [quantize_half(wv00, "wv00", "wd01_codes")]
         g_q = [(g0_codes, g0_scales), quantize(grad1, N, E5M2, "g1")]
-        wv_a.append(quantize_half(wv10, "wv10", "w_sb2"))
+        wv10_codes, wv10_scales = new([P, 2 * P], U32, "wv10_codes", "w_sb2"), new([P, 2 * P], U8, "wv10_scales")
+        for t in range(2):
+            cols = slice(P * t, P * (t + 1))
+            nc.vector.quantize_mx(out=wv10_codes[:, cols].bitcast(E4M3), scales=wv10_scales[:, cols], in_=wv10[:, t].rearrange("p m j -> p (m j)"))
+        wv_a.append((wv10_codes, wv10_scales))
         wv_b = quantize(deal_wv(1, "wd11_scales"), 4 * P, E4M3, "wv_b", "x_codes")
 
-        dx_pair = new([P, 2, N], F32, "dx0", "wd11_scales")
+        dx_pair = new([P, 2, N], F32, "dx0")
         dx_third = new([P, N], F32, "dx2")
         stage = new([P, 2 * T + 256], F32, "stage", "x_codes")
         dx = [dx_pair[:, 0, :], dx_pair[:, 1, :], dx_third[:], stage[:, 2 * T - 256 :]]
@@ -198,7 +202,7 @@ def tile_attend_gml_pl_nce_kernel(tc, xT, wd, wv, y, cw, rw, offs, out_0, out_1,
             nc.vector.tensor_copy(pairs[:, 7, 1, :, t % 2], o_win[t][:, T - 256 :])
 
         words_out = out_1.rearrange("o p c l -> p (o c l)").bitcast(I32)
-        o_scales = new([P, T], U8, "o_scales")
+        o_scales = new([P, T // 2], U8, "o_scales")
         chunks = len(GROUPS)
         reuse = ["x_win0", "x_win1", "x_win2", "x_win3", "s_sb00"]
         woven = [new([P, hi - lo, 256, 2, 2], BF16, "woven%d" % k, tag=reuse[k]) for k, (lo, hi) in enumerate(GROUPS)]
@@ -216,7 +220,7 @@ def tile_attend_gml_pl_nce_kernel(tc, xT, wd, wv, y, cw, rw, offs, out_0, out_1,
 
         def emit(k):
             cols = slice(256 * GROUPS[k][0], 256 * GROUPS[k][1])
-            nc.vector.quantize_mx(out=o_codes[k][:].bitcast(E4M3), scales=o_scales[:, cols], in_=woven[k][:].rearrange("p k c u e -> p (k c u e)"))
+            nc.vector.quantize_mx(out=o_codes[k][:].bitcast(E4M3), scales=o_scales[4 * (cols.start // 1024) :, cols.start % 1024 : cols.start % 1024 + cols.stop - cols.start], in_=woven[k][:].rearrange("p k c u e -> p (k c u e)"))
             nc.sync.dma_start(out=words_out[:, cols], in_=o_codes[k][:].bitcast(I32))
 
         weave(0)
@@ -224,7 +228,7 @@ def tile_attend_gml_pl_nce_kernel(tc, xT, wd, wv, y, cw, rw, offs, out_0, out_1,
             weave(k)
             emit(k - 1)
         emit(chunks - 1)
-        scales_out = out_2.rearrange("o f c -> (o f) c").bitcast(I32)
+        scales_out = out_2.rearrange("o f c -> (o f) c").bitcast(I32).rearrange("f (h c) -> h f c", h=2)
         for q in range(4):
             queue = nc.scalar if q % 2 else nc.sync
-            queue.dma_start(out=scales_out[4 * q : 4 * q + 4, :], in_=o_scales[32 * q : 32 * q + 4, :].bitcast(I32))
+            queue.dma_start(out=scales_out[:, 4 * q : 4 * q + 4, :], in_=o_scales[32 * q : 32 * q + 8, :].bitcast(I32))

@@ -18,8 +18,8 @@ ACT = mybir.ActivationFunctionType
 ALU = mybir.AluOpType
 
 P = 128
-GROUPS = [(7, 8), (0, 2), (2, 4), (4, 6), (6, 7)]
-SPLIT = 5
+GROUPS = [(0, 1), (2, 4), (4, 6), (6, 8), (1, 2)]
+SPLIT = 7
 
 
 def tile_attend_gml_pl_nce_kernel(tc, xT, wd, wv, y, cw, rw, offs, out_0, out_1, out_2):
@@ -64,6 +64,9 @@ def tile_attend_gml_pl_nce_kernel(tc, xT, wd, wv, y, cw, rw, offs, out_0, out_1,
         o_win = [new([P, T], F32, "o_win%d" % t) for t in range(4)]
         for t in range(2):
             nc.vector.memset(o_win[t][:].bitcast(I32), 0)
+        g1_codes, g1_scales = new([P, N], U32, "g1_codes"), new([P, N], U8, "g1_scales")
+        nc.vector.memset(g1_codes[:, N // 2 :], 0)
+        nc.vector.memset(g1_scales[:, N // 2 :].bitcast(U32), 0)
         ident = new([P, P], F32, "ident")
         make_identity(nc, ident[:])
         for t in range(2, 4):
@@ -72,7 +75,7 @@ def tile_attend_gml_pl_nce_kernel(tc, xT, wd, wv, y, cw, rw, offs, out_0, out_1,
         for c in range(4):
             nc.tensor.transpose(rw_bank[:, c, :], rw_sb[:, c : c + 1].to_broadcast([P, P]), ident[:])
         rw_all = rw_bank[:].rearrange("p c n -> p n c")
-        w_cols = [(0, slice(0, 64)), (0, slice(64, 128)), (1, slice(0, 128))]
+        w_cols = [(g, slice(64 * h, 64 * (h + 1))) for g in range(2) for h in range(2)]
         w_sb = [new([P, quads.stop - quads.start, 4, 4], F32, "w_sb%d" % k) for k, (g, quads) in enumerate(w_cols)]
         for k, (g, quads) in enumerate(w_cols):
             for t in range(4):
@@ -89,8 +92,9 @@ def tile_attend_gml_pl_nce_kernel(tc, xT, wd, wv, y, cw, rw, offs, out_0, out_1,
             nc.vector.tensor_copy(x_g[:, :, t], x_win[t][:].indirect(offsets[:]))
         x_q = quantize(x_g[:].rearrange("p n t -> p (n t)"), N, E4M3, "x")
 
-        def deal(raw, h, name, on_vector, tag=None):
-            dealt = new([P, 2, P, 4], BF16, name, tag)
+        def deal(raw, h, name, on_vector, tag=None, dealt=None):
+            if dealt is None:
+                dealt = new([P, 2, P, 4], BF16, name, tag)
             src = raw[:].rearrange("p j (m t) -> p m j t", t=4)[:, :, :, 2 * h : 2 * h + 2]
             dst = dealt[:].rearrange("p t m j -> p m j t")
             if on_vector:
@@ -126,10 +130,11 @@ def tile_attend_gml_pl_nce_kernel(tc, xT, wd, wv, y, cw, rw, offs, out_0, out_1,
                 for cols in halves if (g, k) == (0, 3) else [slice(0, N)]:
                     nc.vector.tensor_tensor(y_sb[g][:, lanes, cols], s_sb[g][k][:, :, cols], y_sb[g][:, lanes, cols], ALU.subtract)
 
-        def weigh(k, tag=None):
+        def weigh(k, tag=None, grad=None):
             g, quads = w_cols[k]
             width = 4 * (quads.stop - quads.start)
-            grad = new([P, width, 4], BF16, "grad%d" % k, tag)
+            if grad is None:
+                grad = new([P, width, 4], BF16, "grad%d" % k, tag)
             nc.vector.tensor_tensor(
                 grad[:].rearrange("p (c i) t -> p c t i", i=4),
                 y_sb[g][:].rearrange("p t (c i) -> p c t i", i=4)[:, quads],
@@ -162,44 +167,62 @@ def tile_attend_gml_pl_nce_kernel(tc, xT, wd, wv, y, cw, rw, offs, out_0, out_1,
             return dealt[:].rearrange("p g t m j -> p (g t m j)")
 
         wv00 = deal(wv_raw[0], 0, "wv00", False, "x_codes")
-        wv10 = deal(wv_raw[1], 0, "wv10", False)
+        shared = new([P, 1536], BF16, "shared")
+        wv10 = deal(wv_raw[1], 0, "wv10", False, dealt=shared[:, 512:].rearrange("p (t m j) -> p t m j", t=2, j=4))
         subtract(1, [0, 1])
         nc.vector.quantize_mx(out=g0_codes[:, halves[1]].bitcast(E5M2), scales=g0_scales[:, halves[1]], in_=grad0b)
-        grad1 = weigh(2)
-        wv_a = [quantize_half(wv00, "wv00", "wd01_codes")]
-        g_q = [(g0_codes, g0_scales), quantize(grad1, N, E5M2, "g1")]
-        wv10_codes, wv10_scales = new([P, 2 * P], U32, "wv10_codes", "w_sb2"), new([P, 2 * P], U8, "wv10_scales")
-        for t in range(2):
-            cols = slice(P * t, P * (t + 1))
-            nc.vector.quantize_mx(out=wv10_codes[:, cols].bitcast(E4M3), scales=wv10_scales[:, cols], in_=wv10[:, t].rearrange("p m j -> p (m j)"))
-        wv_a.append((wv10_codes, wv10_scales))
-        wv_b = quantize(deal_wv(1, "wd11_scales"), 4 * P, E4M3, "wv_b", "x_codes")
+        def quantize_lane(dealt, t, name, tag=None):
+            return quantize(dealt[:, t].rearrange("p m j -> p (m j)"), P, E4M3, name, tag) + (0,)
 
-        dx_pair = new([P, 2, N], F32, "dx0")
-        dx_third = new([P, N], F32, "dx2")
-        stage = new([P, 2 * T + 256], F32, "stage", "x_codes")
-        dx = [dx_pair[:, 0, :], dx_pair[:, 1, :], dx_third[:], stage[:, 2 * T - 256 :]]
-        for h in range(2):
-            banks = [psum.tile([P, N], F32, name="bank") for t in range(2)]
-            for g in range(2):
-                for t in (2 * h, 2 * h + 1):
-                    first = P * (t % 2) + 2 * P * g * h
-                    codes, scales = wv_b if h else wv_a[g]
+        grad1a = weigh(2)
+        wv_q = {(0, 0): quantize_lane(wv00, 0, "wv00", "wd01_codes")}
+        nc.vector.quantize_mx(out=g1_codes[:, halves[0]].bitcast(E5M2), scales=g1_scales[:, halves[0]], in_=grad1a)
+        for t in range(2):
+            wv_q[t, 1] = quantize_lane(wv10, t, "wv1%d" % t)
+        g_q = [(g0_codes, g0_scales), (g1_codes, g1_scales)]
+
+        def product(lanes, passes=(0, 1)):
+            banks = [psum.tile([P, N], F32, name="bank") for t in lanes]
+            for g in passes:
+                for t, bank in zip(lanes, banks):
+                    codes, scales, first = wv_q[t, g]
                     lhs, lhs_s = codes[:, first : first + P].bitcast(E4M3), scales[:, first : first + P]
-                    nc.tensor.matmul_mx(out=banks[t % 2][:], lhsT=lhs, lhsT_scale=lhs_s, rhs=g_q[g][0][:].bitcast(E5M2), rhs_scale=g_q[g][1][:], start=(g == 0), stop=(g == 1))
-            for t in (2 * h, 2 * h + 1):
-                nc.scalar.copy(dx[t], banks[t % 2][:])
+                    nc.tensor.matmul_mx(out=bank[:], lhsT=lhs, lhsT_scale=lhs_s, rhs=g_q[g][0][:].bitcast(E5M2), rhs_scale=g_q[g][1][:], start=(g == passes[0]), stop=(g == passes[1]))
+            return banks
+
+        early = product([0])[0]
+        grad1b = weigh(3, grad=shared[:, :1024].rearrange("p (n t) -> p n t", t=4))
+        wv_b = quantize(deal_wv(1, "wd11_scales"), 4 * P, E4M3, "wv_b", "w_sb2")
+        for g in range(2):
+            for t in (2, 3):
+                wv_q[t, g] = wv_b + (2 * P * g + P * (t - 2),)
+        dx0 = [new([P, N // 2], F32, "dx0%d" % h, None if h else "w_sb3") for h in range(2)]
+        nc.scalar.copy(dx0[0][:], early[:, halves[0]])
+        nc.vector.quantize_mx(out=g1_codes[:, halves[1]].bitcast(E5M2), scales=g1_scales[:, halves[1]], in_=grad1b)
+        nc.vector.tensor_copy(o_win[0][:].indirect(offsets[:, :16]), dx0[0][:])
+        wv_q[1, 0] = quantize_lane(wv00, 1, "wv01", "wd11_scales")
+        nc.scalar.copy(dx0[1][:], product([0])[0][:, halves[1]])
+        dx = {t: new([P, N], F32, "dx%d" % t)[:] for t in (2, 3)}
+        for t, bank in zip((2, 3), product([2, 3])):
+            nc.scalar.copy(dx[t], bank[:])
+        last_bank = product([1], (1, 0))[0]
+        stage = new([P, 2 * T + 256], F32, "stage", "wd11_scales")
+        dx[1] = stage[:, :N]
+        nc.scalar.copy(dx[1], last_bank[:])
 
         out_rows = out_0.rearrange("(p t) c -> t p c", t=4)
-        pairs = stage[:, : 2 * T].bitcast(BF16).rearrange("p (k u c e) -> p k u c e", k=8, u=2, e=2)
-        for t in range(4):
-            nc.vector.tensor_copy(o_win[t][:].indirect(offsets[:]), dx[t])
+        pairs = stage[:, 256:].bitcast(BF16).rearrange("p (k u c e) -> p k u c e", k=8, u=2, e=2)
+        for t in (0, 2, 3, 1):
+            if t:
+                nc.vector.tensor_copy(o_win[t][:].indirect(offsets[:]), dx[t])
+            else:
+                nc.vector.tensor_copy(o_win[0][:].indirect(offsets[:, 16:]), dx0[1][:])
             nc.sync.dma_start(out=out_rows[t], in_=o_win[t][:])
-            for lo, hi in [[(0, 8)], [(0, 8)], [(0, 7)], GROUPS[1:]][t]:
+            for lo, hi in [[(1, 8)], GROUPS[1:], [(0, 8)], [(0, 8)]][t]:
                 nc.scalar.copy(pairs[:, lo:hi, t // 2, :, t % 2], o_win[t][:, 256 * lo : 256 * hi].rearrange("p (k c) -> p k c", c=256))
 
-        for t in (3, 2):
-            nc.vector.tensor_copy(pairs[:, 7, 1, :, t % 2], o_win[t][:, T - 256 :])
+        for t in (1, 0):
+            nc.vector.tensor_copy(pairs[:, 0, 0, :, t], o_win[t][:, :256])
 
         words_out = out_1.rearrange("o p c l -> p (o c l)").bitcast(I32)
         o_scales = new([P, T // 2], U8, "o_scales")
@@ -210,7 +233,7 @@ def tile_attend_gml_pl_nce_kernel(tc, xT, wd, wv, y, cw, rw, offs, out_0, out_1,
 
         def weave(k):
             lo, hi = GROUPS[k]
-            mid = min(max(lo, SPLIT), hi) if k else hi
+            mid = min(SPLIT, hi) if k < chunks - 1 else lo
             dst = woven[k][:].rearrange("p k c u e -> p k c (u e)")
             src = pairs.rearrange("p k u c e -> p k u (c e)")
             if mid > lo:

@@ -18,7 +18,7 @@ ACT = mybir.ActivationFunctionType
 ALU = mybir.AluOpType
 
 P = 128
-GROUPS = [(0, 1), (2, 4), (4, 6), (6, 8), (1, 2)]
+GROUPS = [(0, 1), (2, 4), (4, 6), (6, 7), (7, 8), (1, 2)]
 SPLIT = 7
 
 
@@ -75,7 +75,7 @@ def tile_attend_gml_pl_nce_kernel(tc, xT, wd, wv, y, cw, rw, offs, out_0, out_1,
         for c in range(4):
             nc.tensor.transpose(rw_bank[:, c, :], rw_sb[:, c : c + 1].to_broadcast([P, P]), ident[:])
         rw_all = rw_bank[:].rearrange("p c n -> p n c")
-        w_cols = [(g, slice(64 * h, 64 * (h + 1))) for g in range(2) for h in range(2)]
+        w_cols = [(0, slice(0, 32)), (0, slice(32, 128)), (1, slice(0, 64)), (1, slice(64, 128))]
         w_sb = [new([P, quads.stop - quads.start, 4, 4], F32, "w_sb%d" % k) for k, (g, quads) in enumerate(w_cols)]
         for k, (g, quads) in enumerate(w_cols):
             for t in range(4):
@@ -114,6 +114,7 @@ def tile_attend_gml_pl_nce_kernel(tc, xT, wd, wv, y, cw, rw, offs, out_0, out_1,
         s_lanes = [[slice(t, t + 1) for t in range(4)], [slice(0, 2), slice(2, 4)]]
         s_sb = [[new([P, lanes.stop - lanes.start, N], F32, "s_sb%d%d" % (g, lanes.start)) for lanes in s_lanes[g]] for g in range(2)]
         halves = [slice(0, N // 2), slice(N // 2, N)]
+        parts = [slice(0, P), slice(P, N)]
 
         def scores(g, wd_q):
             for k, lanes in enumerate(s_lanes[g]):
@@ -121,13 +122,13 @@ def tile_attend_gml_pl_nce_kernel(tc, xT, wd, wv, y, cw, rw, offs, out_0, out_1,
                     bank = psum.tile([P, N], F32, name="bank")
                     lhs, lhs_s = stationary(wd_q, t)
                     nc.tensor.matmul_mx(out=bank[:], lhsT=lhs, lhsT_scale=lhs_s, rhs=x_q[0][:].bitcast(E4M3), rhs_scale=x_q[1][:], start=True, stop=True)
-                    for cols in halves if (g, t) == (0, 3) else [slice(0, N)]:
+                    for cols in parts if (g, t) == (0, 3) else [slice(0, N)]:
                         nc.scalar.activation(s_sb[g][k][:, t - lanes.start, cols], bank[:, cols], ACT.Sigmoid)
 
         def subtract(g, ks):
             for k in ks:
                 lanes = s_lanes[g][k]
-                for cols in halves if (g, k) == (0, 3) else [slice(0, N)]:
+                for cols in parts if (g, k) == (0, 3) else [slice(0, N)]:
                     nc.vector.tensor_tensor(y_sb[g][:, lanes, cols], s_sb[g][k][:, :, cols], y_sb[g][:, lanes, cols], ALU.subtract)
 
         def weigh(k, tag=None, grad=None):
@@ -152,11 +153,10 @@ def tile_attend_gml_pl_nce_kernel(tc, xT, wd, wv, y, cw, rw, offs, out_0, out_1,
         wd1_q = [quantize_half(wd10, "wd10")]
         wd11 = deal(wd_raw[1], 1, "wd11", False, "wd01_codes")
         subtract(0, [1, 2, 3])
-        grad0a = weigh(0)
+        grad0 = new([P, N, 4], BF16, "grad0")
+        weigh(0, grad=grad0[:, parts[0]])
         wd1_q.append(quantize_half(wd11, "wd11", "s_sb03"))
-        g0_codes, g0_scales = new([P, N], U32, "g0_codes"), new([P, N], U8, "g0_scales")
-        nc.vector.quantize_mx(out=g0_codes[:, halves[0]].bitcast(E5M2), scales=g0_scales[:, halves[0]], in_=grad0a)
-        grad0b = weigh(1, "wd01_codes")
+        weigh(1, grad=grad0[:, parts[1]])
         scores(1, wd1_q)
 
         def deal_wv(h, tag):
@@ -170,12 +170,13 @@ def tile_attend_gml_pl_nce_kernel(tc, xT, wd, wv, y, cw, rw, offs, out_0, out_1,
         shared = new([P, 1536], BF16, "shared")
         wv10 = deal(wv_raw[1], 0, "wv10", False, dealt=shared[:, 512:].rearrange("p (t m j) -> p t m j", t=2, j=4))
         subtract(1, [0, 1])
-        nc.vector.quantize_mx(out=g0_codes[:, halves[1]].bitcast(E5M2), scales=g0_scales[:, halves[1]], in_=grad0b)
+        g0_codes, g0_scales = quantize(grad0[:].rearrange("p n t -> p (n t)"), N, E5M2, "g0", "s_sb10")
+
         def quantize_lane(dealt, t, name, tag=None):
             return quantize(dealt[:, t].rearrange("p m j -> p (m j)"), P, E4M3, name, tag) + (0,)
 
         grad1a = weigh(2)
-        wv_q = {(0, 0): quantize_lane(wv00, 0, "wv00", "wd01_codes")}
+        wv_q = {(0, 0): quantize_lane(wv00, 0, "wv00", "grad0")}
         nc.vector.quantize_mx(out=g1_codes[:, halves[0]].bitcast(E5M2), scales=g1_scales[:, halves[0]], in_=grad1a)
         for t in range(2):
             wv_q[t, 1] = quantize_lane(wv10, t, "wv1%d" % t)
@@ -218,7 +219,7 @@ def tile_attend_gml_pl_nce_kernel(tc, xT, wd, wv, y, cw, rw, offs, out_0, out_1,
             else:
                 nc.vector.tensor_copy(o_win[0][:].indirect(offsets[:, 16:]), dx0[1][:])
             nc.sync.dma_start(out=out_rows[t], in_=o_win[t][:])
-            for lo, hi in [[(1, 8)], GROUPS[1:], [(0, 8)], [(0, 8)]][t]:
+            for lo, hi in [[(1, 8)], [(2, 4), (4, 6), (6, 8), (1, 2)], [(0, 8)], [(0, 8)]][t]:
                 nc.scalar.copy(pairs[:, lo:hi, t // 2, :, t % 2], o_win[t][:, 256 * lo : 256 * hi].rearrange("p (k c) -> p k c", c=256))
 
         for t in (1, 0):
@@ -227,13 +228,13 @@ def tile_attend_gml_pl_nce_kernel(tc, xT, wd, wv, y, cw, rw, offs, out_0, out_1,
         words_out = out_1.rearrange("o p c l -> p (o c l)").bitcast(I32)
         o_scales = new([P, T // 2], U8, "o_scales")
         chunks = len(GROUPS)
-        reuse = ["x_win0", "x_win1", "x_win2", "x_win3", "s_sb00"]
+        reuse = ["x_win0", "x_win1", "x_win2", "x_win3", "s_sb00", "s_sb01"]
         woven = [new([P, hi - lo, 256, 2, 2], BF16, "woven%d" % k, tag=reuse[k]) for k, (lo, hi) in enumerate(GROUPS)]
         o_codes = [new([P, 256 * (hi - lo)], U32, "o_codes%d" % k) for k, (lo, hi) in enumerate(GROUPS)]
 
         def weave(k):
             lo, hi = GROUPS[k]
-            mid = min(SPLIT, hi) if k < chunks - 1 else lo
+            mid = hi if k < chunks - 2 else lo
             dst = woven[k][:].rearrange("p k c u e -> p k c (u e)")
             src = pairs.rearrange("p k u c e -> p k u (c e)")
             if mid > lo:

@@ -54,8 +54,8 @@ def tile_attend_gml_pl_nce_kernel(tc, xT, wd, wv, y, cw, rw, offs, out_0, out_1,
             nc.sync.dma_start(out=wd_raw[g][:], in_=wd_rows[:, :, 512 * g : 512 * (g + 1)])
         for lanes in (slice(t, t + 1) for t in range(4)):
             nc.sync.dma_start(out=y_sb[0][:, lanes, :], in_=y_rows[0][:, lanes, :])
-        nc.sync.dma_start(out=y_sb[1][:], in_=y_rows[1])
         for g in range(2):
+            nc.sync.dma_start(out=y_sb[1][:, 2 * g : 2 * g + 2, :], in_=y_rows[1][:, 2 * g : 2 * g + 2, :])
             nc.sync.dma_start(out=wv_raw[g][:], in_=wv_rows[g])
 
         warm = new([P, 8], F32, "warm")
@@ -88,9 +88,14 @@ def tile_attend_gml_pl_nce_kernel(tc, xT, wd, wv, y, cw, rw, offs, out_0, out_1,
             return codes, scales
 
         x_g = new([P, N, 4], BF16, "x_g")
-        for t in range(4):
+        for t in range(3):
             nc.vector.tensor_copy(x_g[:, :, t], x_win[t][:].indirect(offsets[:]))
-        x_q = quantize(x_g[:].rearrange("p n t -> p (n t)"), N, E4M3, "x")
+        for h in range(2):
+            nc.vector.tensor_copy(x_g[:, 256 * h : 256 * (h + 1), 3], x_win[3][:].indirect(offsets[:, 16 * h : 16 * (h + 1)]))
+        x_q = (new([P, N], U32, "x_codes"), new([P, N], U8, "x_scales"))
+        for h in range(2):
+            cols = slice(256 * h, 256 * (h + 1))
+            nc.vector.quantize_mx(out=x_q[0][:, cols].bitcast(E4M3), scales=x_q[1][:, cols], in_=x_g[:, cols].rearrange("p n t -> p (n t)"))
 
         def deal(raw, h, name, on_vector, tag=None, dealt=None):
             if dealt is None:
@@ -128,7 +133,7 @@ def tile_attend_gml_pl_nce_kernel(tc, xT, wd, wv, y, cw, rw, offs, out_0, out_1,
         def subtract(g, ks):
             for k in ks:
                 lanes = s_lanes[g][k]
-                for cols in parts if (g, k) == (0, 3) else [slice(0, N)]:
+                for cols in {(0, 3): parts, (1, 1): halves}.get((g, k), [slice(0, N)]):
                     nc.vector.tensor_tensor(y_sb[g][:, lanes, cols], s_sb[g][k][:, :, cols], y_sb[g][:, lanes, cols], ALU.subtract)
 
         def weigh(k, tag=None, grad=None):
@@ -146,7 +151,11 @@ def tile_attend_gml_pl_nce_kernel(tc, xT, wd, wv, y, cw, rw, offs, out_0, out_1,
 
         wd00 = deal(wd_raw[0], 0, "wd00", True)
         wd01 = deal(wd_raw[0], 1, "wd01", False)
-        wd0_q = [quantize_half(wd00, "wd00"), quantize_half(wd01, "wd01")]
+        wd00_q = (new([P, 2 * P], U32, "wd00_codes"), new([P, 2 * P], U8, "wd00_scales"))
+        for t in range(2):
+            cols = slice(P * t, P * (t + 1))
+            nc.vector.quantize_mx(out=wd00_q[0][:, cols].bitcast(E4M3), scales=wd00_q[1][:, cols], in_=wd00[:, t].rearrange("p m j -> p (m j)"))
+        wd0_q = [wd00_q, quantize_half(wd01, "wd01")]
         scores(0, wd0_q)
         wd10 = deal(wd_raw[1], 0, "wd10", True)
         subtract(0, [0])
@@ -159,18 +168,14 @@ def tile_attend_gml_pl_nce_kernel(tc, xT, wd, wv, y, cw, rw, offs, out_0, out_1,
         weigh(1, grad=grad0[:, parts[1]])
         scores(1, wd1_q)
 
-        def deal_wv(h, tag):
-            dealt = new([P, 2, 2, P, 4], BF16, "wv_dealt%d" % h, tag)
-            for g in range(2):
-                src = wv_raw[g][:].rearrange("p j (m t) -> p m j t", t=4)[:, :, :, 2 * h : 2 * h + 2]
-                nc.scalar.copy(dealt[:, g].rearrange("p t m j -> p m j t"), src)
-            return dealt[:].rearrange("p g t m j -> p (g t m j)")
-
-        wv00 = deal(wv_raw[0], 0, "wv00", False, "x_codes")
+        wv_dealt = new([P, 6, P, 4], BF16, "wv_dealt", "x_codes")
+        nc.scalar.copy(wv_dealt[:, :4].rearrange("p t m j -> p m j t"), wv_raw[0][:].rearrange("p j (m t) -> p m j t", t=4))
+        wv00 = wv_dealt[:, :2]
         shared = new([P, 1536], BF16, "shared")
         wv10 = deal(wv_raw[1], 0, "wv10", False, dealt=shared[:, 512:].rearrange("p (t m j) -> p t m j", t=2, j=4))
+        deal(wv_raw[1], 1, "wv11", False, dealt=wv_dealt[:, 4:])
         subtract(1, [0, 1])
-        g0_codes, g0_scales = quantize(grad0[:].rearrange("p n t -> p (n t)"), N, E5M2, "g0", "s_sb10")
+        g0_codes, g0_scales = quantize(grad0[:].rearrange("p n t -> p (n t)"), N, E5M2, "g0")
 
         def quantize_lane(dealt, t, name, tag=None):
             return quantize(dealt[:, t].rearrange("p m j -> p (m j)"), P, E4M3, name, tag) + (0,)
@@ -193,7 +198,7 @@ def tile_attend_gml_pl_nce_kernel(tc, xT, wd, wv, y, cw, rw, offs, out_0, out_1,
 
         early = product([0])[0]
         grad1b = weigh(3, grad=shared[:, :1024].rearrange("p (n t) -> p n t", t=4))
-        wv_b = quantize(deal_wv(1, "wd11_scales"), 4 * P, E4M3, "wv_b", "w_sb2")
+        wv_b = quantize(wv_dealt[:, 2:].rearrange("p t m j -> p (t m j)"), 4 * P, E4M3, "wv_b", "w_sb2")
         for g in range(2):
             for t in (2, 3):
                 wv_q[t, g] = wv_b + (2 * P * g + P * (t - 2),)
@@ -201,13 +206,13 @@ def tile_attend_gml_pl_nce_kernel(tc, xT, wd, wv, y, cw, rw, offs, out_0, out_1,
         nc.scalar.copy(dx0[0][:], early[:, halves[0]])
         nc.vector.quantize_mx(out=g1_codes[:, halves[1]].bitcast(E5M2), scales=g1_scales[:, halves[1]], in_=grad1b)
         nc.vector.tensor_copy(o_win[0][:].indirect(offsets[:, :16]), dx0[0][:])
-        wv_q[1, 0] = quantize_lane(wv00, 1, "wv01", "wd11_scales")
+        wv_q[1, 0] = quantize_lane(wv00, 1, "wv01", "shared")
         nc.scalar.copy(dx0[1][:], product([0])[0][:, halves[1]])
         dx = {t: new([P, N], F32, "dx%d" % t)[:] for t in (2, 3)}
         for t, bank in zip((2, 3), product([2, 3])):
             nc.scalar.copy(dx[t], bank[:])
         last_bank = product([1], (1, 0))[0]
-        stage = new([P, 2 * T + 256], F32, "stage", "wd11_scales")
+        stage = new([P, 2 * T + 256], F32, "stage", "shared")
         dx[1] = stage[:, :N]
         nc.scalar.copy(dx[1], last_bank[:])
 

@@ -224,8 +224,10 @@ def tile_attend_gml_pl_nce_kernel(tc, xT, wd, wv, y, cw, rw, offs, out_0, out_1,
             else:
                 nc.vector.tensor_copy(o_win[0][:].indirect(offsets[:, 16:]), dx0[1][:])
             nc.sync.dma_start(out=out_rows[t], in_=o_win[t][:])
-            for lo, hi in [[(1, 8)], [(2, 4), (4, 6), (6, 8), (1, 2)], [(0, 8)], [(0, 8)]][t]:
+            for lo, hi in [[(1, 8)], [(2, 4), (4, 6), (6, 8), (1, 2)], [(0, 5)], [(0, 5)]][t]:
                 nc.scalar.copy(pairs[:, lo:hi, t // 2, :, t % 2], o_win[t][:, 256 * lo : 256 * hi].rearrange("p (k c) -> p k c", c=256))
+            if t >= 2:
+                nc.gpsimd.tensor_scalar(pairs[:, 5:8, 1, :, t % 2], o_win[t][:, 256 * 5 :].rearrange("p (k c) -> p k c", c=256), 1.0, -0.0, ALU.mult, ALU.add)
 
         for t in (1, 0):
             nc.vector.tensor_copy(pairs[:, 0, 0, :, t], o_win[t][:, :256])

@@ -19,7 +19,8 @@ ALU = mybir.AluOpType
 
 P = 128
 GROUPS = [(0, 1), (2, 4), (4, 6), (6, 7), (7, 8), (1, 2)]
-SPLIT = 7
+OWN = 128
+POOL_STRIP = 4
 
 
 def tile_attend_gml_pl_nce_kernel(tc, xT, wd, wv, y, cw, rw, offs, out_0, out_1, out_2):
@@ -39,7 +40,8 @@ def tile_attend_gml_pl_nce_kernel(tc, xT, wd, wv, y, cw, rw, offs, out_0, out_1,
         rw_sb = new([P, 4], F32, "rw_sb")
         wd_raw = [new([P, 4, 512], F32, "wd_raw%d" % g) for g in range(2)]
         wv_raw = [new([P, 4, 512], F32, "wv_raw%d" % g) for g in range(2)]
-        y_sb = [new([P, 4, N], F32, "y_sb%d" % g) for g in range(2)]
+        y0 = new([P, 4, N], F32, "y0")
+        y1 = [new([P, 4, N // 2], F32, "y1%d" % h) for h in range(2)]
         wd_rows = wd.rearrange("(p j) v -> p j v", j=4)
         wv_rows = wv.rearrange("(g p j) d -> g p j d", g=2, j=4)
         y_rows = y.rearrange("(g p t) i -> g p t i", g=2, t=4)
@@ -53,10 +55,11 @@ def tile_attend_gml_pl_nce_kernel(tc, xT, wd, wv, y, cw, rw, offs, out_0, out_1,
         for g in range(2):
             nc.sync.dma_start(out=wd_raw[g][:], in_=wd_rows[:, :, 512 * g : 512 * (g + 1)])
         for lanes in (slice(t, t + 1) for t in range(4)):
-            nc.sync.dma_start(out=y_sb[0][:, lanes, :], in_=y_rows[0][:, lanes, :])
+            nc.sync.dma_start(out=y0[:, lanes, :], in_=y_rows[0][:, lanes, :])
+        nc.sync.dma_start(out=y1[0][:], in_=y_rows[1][:, :, : N // 2])
         for g in range(2):
-            nc.sync.dma_start(out=y_sb[1][:, 2 * g : 2 * g + 2, :], in_=y_rows[1][:, 2 * g : 2 * g + 2, :])
             nc.sync.dma_start(out=wv_raw[g][:], in_=wv_rows[g])
+        nc.sync.dma_start(out=y1[1][:], in_=y_rows[1][:, :, N // 2 :])
 
         warm = new([P, 8], F32, "warm")
         nc.vector.memset(warm[:, 0:1], 0.0)
@@ -75,7 +78,7 @@ def tile_attend_gml_pl_nce_kernel(tc, xT, wd, wv, y, cw, rw, offs, out_0, out_1,
         for c in range(4):
             nc.tensor.transpose(rw_bank[:, c, :], rw_sb[:, c : c + 1].to_broadcast([P, P]), ident[:])
         rw_all = rw_bank[:].rearrange("p c n -> p n c")
-        w_cols = [(0, slice(0, 32)), (0, slice(32, 128)), (1, slice(0, 64)), (1, slice(64, 128))]
+        w_cols = [(0, slice(0, 32)), (0, slice(32, 128)), (1, slice(0, 64)), (1, slice(64, 64 + OWN // 4)), (1, slice(64 + OWN // 4, 128))]
         w_sb = [new([P, quads.stop - quads.start, 4, 4], F32, "w_sb%d" % k) for k, (g, quads) in enumerate(w_cols)]
         for k, (g, quads) in enumerate(w_cols):
             for t in range(4):
@@ -117,37 +120,39 @@ def tile_attend_gml_pl_nce_kernel(tc, xT, wd, wv, y, cw, rw, offs, out_0, out_1,
             return codes[:, cols].bitcast(E4M3), scales[:, cols]
 
         s_lanes = [[slice(t, t + 1) for t in range(4)], [slice(0, 2), slice(2, 4)]]
-        s_sb = [[new([P, lanes.stop - lanes.start, N], F32, "s_sb%d%d" % (g, lanes.start)) for lanes in s_lanes[g]] for g in range(2)]
+        s1 = new([P, 4, N // 2], F32, "s1")
+        s_sb = [[new([P, 1, N], F32, "s_sb0%d" % t) for t in range(4)], [s1[:, :2], s1[:, 2:]]]
         halves = [slice(0, N // 2), slice(N // 2, N)]
         parts = [slice(0, P), slice(P, N)]
 
         def scores(g, wd_q):
+            banks = []
             for k, lanes in enumerate(s_lanes[g]):
                 for t in range(lanes.start, lanes.stop):
                     bank = psum.tile([P, N], F32, name="bank")
                     lhs, lhs_s = stationary(wd_q, t)
                     nc.tensor.matmul_mx(out=bank[:], lhsT=lhs, lhsT_scale=lhs_s, rhs=x_q[0][:].bitcast(E4M3), rhs_scale=x_q[1][:], start=True, stop=True)
-                    for cols in parts if (g, t) == (0, 3) else [slice(0, N)]:
+                    banks.append(bank)
+                    for cols in [halves[0]] if g else parts if t == 3 else [slice(0, N)]:
                         nc.scalar.activation(s_sb[g][k][:, t - lanes.start, cols], bank[:, cols], ACT.Sigmoid)
+            return banks
 
-        def subtract(g, ks):
-            for k in ks:
-                lanes = s_lanes[g][k]
-                for cols in {(0, 3): parts, (1, 1): halves}.get((g, k), [slice(0, N)]):
-                    nc.vector.tensor_tensor(y_sb[g][:, lanes, cols], s_sb[g][k][:, :, cols], y_sb[g][:, lanes, cols], ALU.subtract)
+        def subtract0(k):
+            lanes = s_lanes[0][k]
+            for cols in parts if k == 3 else [slice(0, N)]:
+                nc.vector.tensor_tensor(y0[:, lanes, cols], s_sb[0][k][:, :, cols], y0[:, lanes, cols], ALU.subtract)
 
-        def weigh(k, tag=None, grad=None):
-            g, quads = w_cols[k]
-            width = 4 * (quads.stop - quads.start)
-            if grad is None:
-                grad = new([P, width, 4], BF16, "grad%d" % k, tag)
-            nc.vector.tensor_tensor(
-                grad[:].rearrange("p (c i) t -> p c t i", i=4),
-                y_sb[g][:].rearrange("p t (c i) -> p c t i", i=4)[:, quads],
+        def subtract1(h, s_half, lanes, cols, out=None):
+            y_part = y1[h][:, lanes, cols]
+            nc.vector.tensor_tensor(y_part if out is None else out, s_half[:, lanes, cols], y_part, ALU.subtract)
+
+        def weigh(k, diff, grad, engine=nc.vector):
+            engine.tensor_tensor(
+                grad.rearrange("p (c i) t -> p c t i", i=4),
+                diff.rearrange("p t (c i) -> p c t i", i=4),
                 w_sb[k][:],
                 ALU.mult,
             )
-            return grad[:].rearrange("p n t -> p (n t)")
 
         wd00 = deal(wd_raw[0], 0, "wd00", True)
         wd01 = deal(wd_raw[0], 1, "wd01", False)
@@ -158,76 +163,86 @@ def tile_attend_gml_pl_nce_kernel(tc, xT, wd, wv, y, cw, rw, offs, out_0, out_1,
         wd0_q = [wd00_q, quantize_half(wd01, "wd01")]
         scores(0, wd0_q)
         wd10 = deal(wd_raw[1], 0, "wd10", True)
-        subtract(0, [0])
+        subtract0(0)
         wd1_q = [quantize_half(wd10, "wd10")]
         wd11 = deal(wd_raw[1], 1, "wd11", False, "wd01_codes")
-        subtract(0, [1, 2, 3])
+        for k in (1, 2, 3):
+            subtract0(k)
         grad0 = new([P, N, 4], BF16, "grad0")
-        weigh(0, grad=grad0[:, parts[0]])
+        weigh(0, y0[:, :, parts[0]], grad0[:, parts[0]])
         wd1_q.append(quantize_half(wd11, "wd11", "s_sb03"))
-        weigh(1, grad=grad0[:, parts[1]])
-        scores(1, wd1_q)
+        weigh(1, y0[:, :, parts[1]], grad0[:, parts[1]])
+        banks1 = scores(1, wd1_q)
 
-        wv_dealt = new([P, 6, P, 4], BF16, "wv_dealt", "x_codes")
-        nc.scalar.copy(wv_dealt[:, :4].rearrange("p t m j -> p m j t"), wv_raw[0][:].rearrange("p j (m t) -> p m j t", t=4))
-        wv00 = wv_dealt[:, :2]
-        shared = new([P, 1536], BF16, "shared")
-        wv10 = deal(wv_raw[1], 0, "wv10", False, dealt=shared[:, 512:].rearrange("p (t m j) -> p t m j", t=2, j=4))
-        deal(wv_raw[1], 1, "wv11", False, dealt=wv_dealt[:, 4:])
-        subtract(1, [0, 1])
+        wv0a = deal(wv_raw[0], 1, "wv0a", False, "x_codes")
+        wv1a = deal(wv_raw[1], 1, "wv1a", False)
+        s1b = new([P, 4, N // 2], F32, "s1b")
+        for t in range(4):
+            nc.scalar.activation(s1b[:, t], banks1[t][:, halves[1]], ACT.Sigmoid)
+        mine, pools = slice(0, OWN), slice(OWN, N // 2)
+        subtract1(0, s1, slice(0, 2), halves[0])
+        subtract1(0, s1, slice(2, 4), halves[0])
         g0_codes, g0_scales = quantize(grad0[:].rearrange("p n t -> p (n t)"), N, E5M2, "g0")
+        grad1 = new([P, N // 2, 4], BF16, "grad1")
+        weigh(2, y1[0][:], grad1[:])
+        wv0a_q = quantize_half(wv0a, "wv0a", "grad0")
 
-        def quantize_lane(dealt, t, name, tag=None):
-            return quantize(dealt[:, t].rearrange("p m j -> p (m j)"), P, E4M3, name, tag) + (0,)
+        def quantize_g1(grad, first):
+            cols = slice(first, first + grad.shape[1])
+            nc.vector.quantize_mx(out=g1_codes[:, cols].bitcast(E5M2), scales=g1_scales[:, cols], in_=grad.rearrange("p n t -> p (n t)"))
 
-        grad1a = weigh(2)
-        wv_q = {(0, 0): quantize_lane(wv00, 0, "wv00", "grad0")}
-        nc.vector.quantize_mx(out=g1_codes[:, halves[0]].bitcast(E5M2), scales=g1_scales[:, halves[0]], in_=grad1a)
-        for t in range(2):
-            wv_q[t, 1] = quantize_lane(wv10, t, "wv1%d" % t)
+        quantize_g1(grad1[:], 0)
+        wv1a_q = quantize_half(wv1a, "wv1a")
+        wv_q = {}
+        for t in (2, 3):
+            wv_q[t, 0] = wv0a_q + (P * (t - 2),)
+            wv_q[t, 1] = wv1a_q + (P * (t - 2),)
         g_q = [(g0_codes, g0_scales), (g1_codes, g1_scales)]
 
-        def product(lanes, passes=(0, 1)):
-            banks = [psum.tile([P, N], F32, name="bank") for t in lanes]
+        def product(t, passes=(0, 1)):
+            bank = psum.tile([P, N], F32, name="bank")
             for g in passes:
-                for t, bank in zip(lanes, banks):
-                    codes, scales, first = wv_q[t, g]
-                    lhs, lhs_s = codes[:, first : first + P].bitcast(E4M3), scales[:, first : first + P]
-                    nc.tensor.matmul_mx(out=bank[:], lhsT=lhs, lhsT_scale=lhs_s, rhs=g_q[g][0][:].bitcast(E5M2), rhs_scale=g_q[g][1][:], start=(g == passes[0]), stop=(g == passes[1]))
-            return banks
+                codes, scales, first = wv_q[t, g]
+                lhs, lhs_s = codes[:, first : first + P].bitcast(E4M3), scales[:, first : first + P]
+                nc.tensor.matmul_mx(out=bank[:], lhsT=lhs, lhsT_scale=lhs_s, rhs=g_q[g][0][:].bitcast(E5M2), rhs_scale=g_q[g][1][:], start=(g == passes[0]), stop=(g == passes[1]))
+            return bank
 
-        early = product([0])[0]
-        grad1b = weigh(3, grad=shared[:, :1024].rearrange("p (n t) -> p n t", t=4))
-        wv_b = quantize(wv_dealt[:, 2:].rearrange("p t m j -> p (t m j)"), 4 * P, E4M3, "wv_b", "w_sb2")
+        early = {2: product(2), 3: product(3, (1, 0))}
+        diff = new([P, 4, N // 2], F32, "diff", "wv1a")
+        subtract1(1, s1b, slice(0, 4), halves[0], diff[:])
+        grad_pool = new([P, N // 2 - OWN, 4], BF16, "grad_pool")
+        weigh(4, diff[:, :, pools], grad_pool[:], nc.gpsimd)
+        dx_a = {2: new([P, N // 2], F32, "dx_a2")}
+        nc.scalar.copy(dx_a[2][:], early[2][:, halves[0]])
+        wv0b = deal(wv_raw[0], 0, "wv0b", False, "y11")
+        nc.vector.tensor_copy(o_win[2][:].indirect(offsets[:, :16]), dx_a[2][:])
+        grad_mine = new([P, OWN, 4], BF16, "grad_mine", "w_sb4")
+        weigh(3, diff[:, :, mine], grad_mine[:])
+        dx_a[3] = new([P, N // 2], F32, "dx_a3", "w_sb3")
+        nc.scalar.copy(dx_a[3][:], early[3][:, halves[0]])
+        wv1b = deal(wv_raw[1], 0, "wv1b", False, "wv1a")
+        quantize_g1(grad_pool[:], N // 2 + OWN)
+        wv_b_q = [quantize_half(wv0b, "wv0b")]
+        quantize_g1(grad_mine[:], N // 2)
+        nc.vector.tensor_copy(o_win[3][:].indirect(offsets[:, :16]), dx_a[3][:])
+        wv_b_q.append(quantize_half(wv1b, "wv1b"))
         for g in range(2):
-            for t in (2, 3):
-                wv_q[t, g] = wv_b + (2 * P * g + P * (t - 2),)
-        dx0 = [new([P, N // 2], F32, "dx0%d" % h, None if h else "w_sb3") for h in range(2)]
-        nc.scalar.copy(dx0[0][:], early[:, halves[0]])
-        nc.vector.quantize_mx(out=g1_codes[:, halves[1]].bitcast(E5M2), scales=g1_scales[:, halves[1]], in_=grad1b)
-        nc.vector.tensor_copy(o_win[0][:].indirect(offsets[:, :16]), dx0[0][:])
-        wv_q[1, 0] = quantize_lane(wv00, 1, "wv01", "shared")
-        nc.scalar.copy(dx0[1][:], product([0])[0][:, halves[1]])
-        dx = {t: new([P, N], F32, "dx%d" % t)[:] for t in (2, 3)}
-        for t, bank in zip((2, 3), product([2, 3])):
-            nc.scalar.copy(dx[t], bank[:])
-        last_bank = product([1], (1, 0))[0]
-        stage = new([P, 2 * T + 256], F32, "stage", "shared")
-        dx[1] = stage[:, :N]
-        nc.scalar.copy(dx[1], last_bank[:])
+            for t in (0, 1):
+                wv_q[t, g] = wv_b_q[g] + (P * t,)
+        stage = new([P, 2 * T + 256], F32, "stage", "wv1b_codes")
+        dx = {2: new([P, N // 2], F32, "dx2", "wv_raw1")[:], 0: new([P, N], F32, "dx0")[:], 3: new([P, N // 2], F32, "dx3")[:], 1: stage[:, :N]}
+        for t in (2, 3, 0, 1):
+            nc.scalar.copy(dx[t], product(t, (1, 0) if t >= 2 else (0, 1))[:, halves[1] if t >= 2 else slice(0, N)])
 
         out_rows = out_0.rearrange("(p t) c -> t p c", t=4)
         pairs = stage[:, 256:].bitcast(BF16).rearrange("p (k u c e) -> p k u c e", k=8, u=2, e=2)
-        for t in (0, 2, 3, 1):
-            if t:
-                nc.vector.tensor_copy(o_win[t][:].indirect(offsets[:]), dx[t])
-            else:
-                nc.vector.tensor_copy(o_win[0][:].indirect(offsets[:, 16:]), dx0[1][:])
+        for t in (2, 3, 0, 1):
+            nc.vector.tensor_copy(o_win[t][:].indirect(offsets[:, 16:] if t >= 2 else offsets[:]), dx[t])
             nc.sync.dma_start(out=out_rows[t], in_=o_win[t][:])
-            for lo, hi in [[(1, 8)], [(2, 4), (4, 6), (6, 8), (1, 2)], [(0, 5)], [(0, 5)]][t]:
+            for lo, hi in [[(1, 8)], [(2, 4), (4, 6), (6, 8), (1, 2)], [(0, POOL_STRIP)], [(0, POOL_STRIP)]][t]:
                 nc.scalar.copy(pairs[:, lo:hi, t // 2, :, t % 2], o_win[t][:, 256 * lo : 256 * hi].rearrange("p (k c) -> p k c", c=256))
             if t >= 2:
-                nc.gpsimd.tensor_scalar(pairs[:, 5:8, 1, :, t % 2], o_win[t][:, 256 * 5 :].rearrange("p (k c) -> p k c", c=256), 1.0, -0.0, ALU.mult, ALU.add)
+                nc.gpsimd.tensor_scalar(pairs[:, POOL_STRIP:, 1, :, t % 2], o_win[t][:, 256 * POOL_STRIP :].rearrange("p (k c) -> p k c", c=256), 1.0, -0.0, ALU.mult, ALU.add)
 
         for t in (1, 0):
             nc.vector.tensor_copy(pairs[:, 0, 0, :, t], o_win[t][:, :256])
@@ -261,5 +276,4 @@ def tile_attend_gml_pl_nce_kernel(tc, xT, wd, wv, y, cw, rw, offs, out_0, out_1,
         emit(chunks - 1)
         scales_out = out_2.rearrange("o f c -> (o f) c").bitcast(I32).rearrange("f (h c) -> h f c", h=2)
         for q in range(4):
-            queue = nc.scalar if q % 2 else nc.sync
-            queue.dma_start(out=scales_out[:, 4 * q : 4 * q + 4, :], in_=o_scales[32 * q : 32 * q + 8, :].bitcast(I32))
+            nc.sync.dma_start(out=scales_out[:, 4 * q : 4 * q + 4, :], in_=o_scales[32 * q : 32 * q + 8, :].bitcast(I32))

@@ -18,9 +18,11 @@ ACT = mybir.ActivationFunctionType
 ALU = mybir.AluOpType
 
 P = 128
-GROUPS = [(0, 1), (2, 4), (4, 6), (6, 7), (7, 8), (1, 2)]
+GROUPS = [(0, 2), (2, 4), (4, 6), (6, 7), (7, 8)]
+DIRECT = 2
+WEAVE_SPLIT = 5
 OWN = 128
-POOL_STRIP = 4
+POOL_STRIP = 6
 
 
 def tile_attend_gml_pl_nce_kernel(tc, xT, wd, wv, y, cw, rw, offs, out_0, out_1, out_2):
@@ -229,51 +231,63 @@ def tile_attend_gml_pl_nce_kernel(tc, xT, wd, wv, y, cw, rw, offs, out_0, out_1,
         for g in range(2):
             for t in (0, 1):
                 wv_q[t, g] = wv_b_q[g] + (P * t,)
-        stage = new([P, 2 * T + 256], F32, "stage", "wv1b_codes")
+        stage = new([P, N + 256 * 2 * (8 - DIRECT)], F32, "stage", "wv1b_codes")
         dx = {2: new([P, N // 2], F32, "dx2", "wv_raw1")[:], 0: new([P, N], F32, "dx0")[:], 3: new([P, N // 2], F32, "dx3")[:], 1: stage[:, :N]}
         for t in (2, 3, 0, 1):
             nc.scalar.copy(dx[t], product(t, (1, 0) if t >= 2 else (0, 1))[:, halves[1] if t >= 2 else slice(0, N)])
 
         out_rows = out_0.rearrange("(p t) c -> t p c", t=4)
-        pairs = stage[:, 256:].bitcast(BF16).rearrange("p (k u c e) -> p k u c e", k=8, u=2, e=2)
+        pairs = stage[:, N:].bitcast(BF16).rearrange("p (k u c e) -> p k u c e", k=8 - DIRECT, u=2, e=2)
+        chunks = len(GROUPS)
+        reuse = [None, "x_win1", "x_win2", "x_win3", "x_win0"]
+        woven = [new([P, hi - lo, 256, 2, 2], BF16, "woven%d" % k, tag=reuse[k]) for k, (lo, hi) in enumerate(GROUPS)]
+        direct = woven[0][:].rearrange("p k c u e -> p (k c) (u e)")
+        one = direct[:, 0, 1:2]
+        nc.gpsimd.memset(one, 1.0)
+
+        def strips(t, lo, hi):
+            return pairs[:, lo - DIRECT : hi - DIRECT, t // 2, :, t % 2], o_win[t][:, 256 * lo : 256 * hi].rearrange("p (k c) -> p k c", c=256)
+
+        def weave(lo, hi, k):
+            first = GROUPS[k][0]
+            dst = woven[k][:, lo - first : hi - first].rearrange("p k c u e -> p k c (u e)")
+            src = pairs[:, lo - DIRECT : hi - DIRECT].rearrange("p k u c e -> p k u (c e)")
+            if lo < WEAVE_SPLIT:
+                nc.vector.tensor_copy(dst.bitcast(I32), src.bitcast(I32).rearrange("p k u c -> p k c u"))
+            else:
+                nc.scalar.copy(dst.bitcast(U32), src.bitcast(U32).rearrange("p k u c -> p k c u"))
+
         for t in (2, 3, 0, 1):
             nc.vector.tensor_copy(o_win[t][:].indirect(offsets[:, 16:] if t >= 2 else offsets[:]), dx[t])
             nc.sync.dma_start(out=out_rows[t], in_=o_win[t][:])
-            for lo, hi in [[(1, 8)], [(2, 4), (4, 6), (6, 8), (1, 2)], [(0, POOL_STRIP)], [(0, POOL_STRIP)]][t]:
-                nc.scalar.copy(pairs[:, lo:hi, t // 2, :, t % 2], o_win[t][:, 256 * lo : 256 * hi].rearrange("p (k c) -> p k c", c=256))
-            if t >= 2:
-                nc.gpsimd.tensor_scalar(pairs[:, POOL_STRIP:, 1, :, t % 2], o_win[t][:, 256 * POOL_STRIP :].rearrange("p (k c) -> p k c", c=256), 1.0, -0.0, ALU.mult, ALU.add)
+            if t == 1:
+                break
+            nc.scalar.copy(*strips(t, DIRECT, POOL_STRIP if t else 8))
+            if t:
+                nc.gpsimd.tensor_scalar(*strips(t, POOL_STRIP, 8), 1.0, -0.0, ALU.mult, ALU.add)
+            nc.gpsimd.tensor_scalar(direct[:, :, t], o_win[t][:, : 256 * DIRECT], 1.0 if t else one, -0.0, ALU.mult, ALU.add)
 
-        for t in (1, 0):
-            nc.vector.tensor_copy(pairs[:, 0, 0, :, t], o_win[t][:, :256])
+        nc.vector.tensor_copy(direct[:, :, 1], o_win[1][:, : 256 * DIRECT])
+        nc.scalar.copy(*strips(1, 2, 4))
+        for k in range(4, 8):
+            nc.scalar.copy(*strips(1, k, k + 1))
+            if k >= WEAVE_SPLIT:
+                weave(k, k + 1, {5: 2, 6: 3, 7: 4}[k])
 
         words_out = out_1.rearrange("o p c l -> p (o c l)").bitcast(I32)
         o_scales = new([P, T // 2], U8, "o_scales")
-        chunks = len(GROUPS)
-        reuse = ["x_win0", "x_win1", "x_win2", "x_win3", "s_sb00", "s_sb01"]
-        woven = [new([P, hi - lo, 256, 2, 2], BF16, "woven%d" % k, tag=reuse[k]) for k, (lo, hi) in enumerate(GROUPS)]
         o_codes = [new([P, 256 * (hi - lo)], U32, "o_codes%d" % k) for k, (lo, hi) in enumerate(GROUPS)]
-
-        def weave(k):
-            lo, hi = GROUPS[k]
-            mid = hi if k < chunks - 2 else lo
-            dst = woven[k][:].rearrange("p k c u e -> p k c (u e)")
-            src = pairs.rearrange("p k u c e -> p k u (c e)")
-            if mid > lo:
-                nc.vector.tensor_copy(dst[:, : mid - lo].bitcast(I32), src[:, lo:mid].bitcast(I32).rearrange("p k u c -> p k c u"))
-            if hi > mid:
-                nc.scalar.copy(dst[:, mid - lo :].bitcast(U32), src[:, mid:hi].bitcast(U32).rearrange("p k u c -> p k c u"))
 
         def emit(k):
             cols = slice(256 * GROUPS[k][0], 256 * GROUPS[k][1])
             nc.vector.quantize_mx(out=o_codes[k][:].bitcast(E4M3), scales=o_scales[4 * (cols.start // 1024) :, cols.start % 1024 : cols.start % 1024 + cols.stop - cols.start], in_=woven[k][:].rearrange("p k c u e -> p (k c u e)"))
             nc.sync.dma_start(out=words_out[:, cols], in_=o_codes[k][:].bitcast(I32))
 
-        weave(0)
+        weave(2, 4, 1)
+        emit(0)
+        weave(4, 5, 2)
         for k in range(1, chunks):
-            weave(k)
-            emit(k - 1)
-        emit(chunks - 1)
+            emit(k)
         scales_out = out_2.rearrange("o f c -> (o f) c").bitcast(I32).rearrange("f (h c) -> h f c", h=2)
         for q in range(4):
             nc.sync.dma_start(out=scales_out[:, 4 * q : 4 * q + 4, :], in_=o_scales[32 * q : 32 * q + 8, :].bitcast(I32))

@@ -41,7 +41,7 @@ def tile_attend_gml_pl_nce_kernel(tc, xT, wd, wv, y, cw, rw, offs, out_0, out_1,
         cw_sb = new([P, 2, 4], F32, "cw_sb")
         rw_sb = new([P, 4], F32, "rw_sb")
         wd_raw = [new([P, 4, 512], F32, "wd_raw%d" % g) for g in range(2)]
-        wv_raw = [new([P, 4, 512], F32, "wv_raw%d" % g) for g in range(2)]
+        wv_raw = [new([P, 4, 512], F32, "wv_raw0"), [new([P, 4, 256], F32, "wv_raw1%d" % h) for h in range(2)]]
         y0 = new([P, 4, N], F32, "y0")
         y1 = [new([P, 4, N // 2], F32, "y1%d" % h) for h in range(2)]
         wd_rows = wd.rearrange("(p j) v -> p j v", j=4)
@@ -59,8 +59,9 @@ def tile_attend_gml_pl_nce_kernel(tc, xT, wd, wv, y, cw, rw, offs, out_0, out_1,
         for lanes in (slice(t, t + 1) for t in range(4)):
             nc.sync.dma_start(out=y0[:, lanes, :], in_=y_rows[0][:, lanes, :])
         nc.sync.dma_start(out=y1[0][:], in_=y_rows[1][:, :, : N // 2])
-        for g in range(2):
-            nc.sync.dma_start(out=wv_raw[g][:], in_=wv_rows[g])
+        nc.sync.dma_start(out=wv_raw[0][:], in_=wv_rows[0])
+        for h in range(2):
+            nc.sync.dma_start(out=wv_raw[1][h][:], in_=wv_rows[1][:, :, 256 * h : 256 * (h + 1)])
         nc.sync.dma_start(out=y1[1][:], in_=y_rows[1][:, :, N // 2 :])
 
         warm = new([P, 8], F32, "warm")
@@ -105,12 +106,14 @@ def tile_attend_gml_pl_nce_kernel(tc, xT, wd, wv, y, cw, rw, offs, out_0, out_1,
         def deal(raw, h, name, on_vector, tag=None, dealt=None):
             if dealt is None:
                 dealt = new([P, 2, P, 4], BF16, name, tag)
-            src = raw[:].rearrange("p j (m t) -> p m j t", t=4)[:, :, :, 2 * h : 2 * h + 2]
-            dst = dealt[:].rearrange("p t m j -> p m j t")
-            if on_vector:
-                nc.vector.tensor_copy(dst, src)
-            else:
-                nc.scalar.copy(dst, src)
+            pieces = raw if isinstance(raw, list) else [raw]
+            for k, piece in enumerate(pieces):
+                src = piece[:].rearrange("p j (m t) -> p m j t", t=4)[:, :, :, 2 * h : 2 * h + 2]
+                dst = dealt[:].rearrange("p t m j -> p m j t")[:, P // len(pieces) * k : P // len(pieces) * (k + 1)]
+                if on_vector:
+                    nc.vector.tensor_copy(dst, src)
+                else:
+                    nc.scalar.copy(dst, src)
             return dealt
 
         def quantize_half(dealt, name, tag=None):
@@ -174,13 +177,20 @@ def tile_attend_gml_pl_nce_kernel(tc, xT, wd, wv, y, cw, rw, offs, out_0, out_1,
         weigh(0, y0[:, :, parts[0]], grad0[:, parts[0]])
         wd1_q.append(quantize_half(wd11, "wd11", "s_sb03"))
         weigh(1, y0[:, :, parts[1]], grad0[:, parts[1]])
-        banks1 = scores(1, wd1_q)
+        banks1 = {}
+        for k in range(2):
+            for h in range(2):
+                banks1[k, h] = psum.tile([P, 2, N // 2], F32, name="bank")
+                for e in range(2):
+                    lhs, lhs_s = stationary(wd1_q, 2 * k + e)
+                    nc.tensor.matmul_mx(out=banks1[k, h][:, e], lhsT=lhs, lhsT_scale=lhs_s, rhs=x_q[0][:, halves[h]].bitcast(E4M3), rhs_scale=x_q[1][:, halves[h]], start=True, stop=True)
+            nc.scalar.activation(s1[:, 2 * k : 2 * k + 2], banks1[k, 0][:], ACT.Sigmoid)
 
         wv0a = deal(wv_raw[0], 1, "wv0a", False, "x_codes")
         wv1a = deal(wv_raw[1], 1, "wv1a", False)
         s1b = new([P, 4, N // 2], F32, "s1b")
-        for t in range(4):
-            nc.scalar.activation(s1b[:, t], banks1[t][:, halves[1]], ACT.Sigmoid)
+        for k in range(2):
+            nc.scalar.activation(s1b[:, 2 * k : 2 * k + 2], banks1[k, 1][:], ACT.Sigmoid)
         mine, pools = slice(0, OWN), slice(OWN, N // 2)
         subtract1(0, s1, slice(0, 2), halves[0])
         subtract1(0, s1, slice(2, 4), halves[0])
@@ -232,7 +242,7 @@ def tile_attend_gml_pl_nce_kernel(tc, xT, wd, wv, y, cw, rw, offs, out_0, out_1,
             for t in (0, 1):
                 wv_q[t, g] = wv_b_q[g] + (P * t,)
         stage = new([P, N + 256 * 2 * (8 - DIRECT)], F32, "stage", "wv1b_codes")
-        dx = {2: new([P, N // 2], F32, "dx2", "wv_raw1")[:], 0: new([P, N], F32, "dx0")[:], 3: new([P, N // 2], F32, "dx3")[:], 1: stage[:, :N]}
+        dx = {2: new([P, N // 2], F32, "dx2", "wv_raw11")[:], 0: new([P, N], F32, "dx0")[:], 3: new([P, N // 2], F32, "dx3")[:], 1: stage[:, :N]}
         for t in (2, 3, 0, 1):
             nc.scalar.copy(dx[t], product(t, (1, 0) if t >= 2 else (0, 1))[:, halves[1] if t >= 2 else slice(0, N)])
 
@@ -269,10 +279,12 @@ def tile_attend_gml_pl_nce_kernel(tc, xT, wd, wv, y, cw, rw, offs, out_0, out_1,
 
         nc.vector.tensor_copy(direct[:, :, 1], o_win[1][:, : 256 * DIRECT])
         nc.scalar.copy(*strips(1, 2, 4))
-        for k in range(4, 8):
-            nc.scalar.copy(*strips(1, k, k + 1))
-            if k >= WEAVE_SPLIT:
-                weave(k, k + 1, {5: 2, 6: 3, 7: 4}[k])
+        nc.scalar.copy(*strips(1, 4, 6))
+        nc.scalar.copy(*strips(1, 6, 7))
+        weave(5, 6, 2)
+        nc.scalar.copy(*strips(1, 7, 8))
+        weave(6, 7, 3)
+        weave(7, 8, 4)
 
         words_out = out_1.rearrange("o p c l -> p (o c l)").bitcast(I32)
         o_scales = new([P, T // 2], U8, "o_scales")

@@ -18,11 +18,8 @@ ACT = mybir.ActivationFunctionType
 ALU = mybir.AluOpType
 
 P = 128
-GROUPS = [(0, 2), (2, 4), (4, 6), (6, 7), (7, 8)]
-DIRECT = 2
-WEAVE_SPLIT = 5
-OWN = 128
-POOL_STRIP = 6
+HALF = N // 2
+A, B = 0, 1
 
 
 def tile_attend_gml_pl_nce_kernel(tc, xT, wd, wv, y, cw, rw, offs, out_0, out_1, out_2):
@@ -35,18 +32,23 @@ def tile_attend_gml_pl_nce_kernel(tc, xT, wd, wv, y, cw, rw, offs, out_0, out_1,
         def new(shape, dtype, name, tag=None):
             return sb.tile(shape, dtype, name=name, tag=tag or name, align_bytes=64)
 
+        halves = [slice(0, HALF), slice(HALF, N)]
+        half_offsets = [slice(0, HALF // 16), slice(HALF // 16, N // 16)]
+
         x_rows = xT.rearrange("(p t) c -> t p c", t=4)
         x_win = [new([P, T], F32, "x_win%d" % t) for t in range(4)]
         offsets = lists.tile([P, N // 16], U16, name="offsets")
         cw_sb = new([P, 2, 4], F32, "cw_sb")
         rw_sb = new([P, 4], F32, "rw_sb")
-        wd_raw = [new([P, 4, 512], F32, "wd_raw%d" % g) for g in range(2)]
-        wv_raw = [new([P, 4, 512], F32, "wv_raw0"), [new([P, 4, 256], F32, "wv_raw1%d" % h) for h in range(2)]]
-        y0 = new([P, 4, N], F32, "y0")
-        y1 = [new([P, 4, N // 2], F32, "y1%d" % h) for h in range(2)]
+        wd_raw = [[new([P, 4, 256], F32, "wd_raw0%d" % h) for h in range(2)], [new([P, 4, 512], F32, "wd_raw1")]]
+        wv_raw = [[new([P, 4, 512], F32, "wv_raw%d" % g)] for g in range(2)]
+        y_sb = {(g, h): new([P, 4, HALF], F32, "y%d%d" % (g, h)) for g in range(2) for h in range(2)}
         wd_rows = wd.rearrange("(p j) v -> p j v", j=4)
         wv_rows = wv.rearrange("(g p j) d -> g p j d", g=2, j=4)
         y_rows = y.rearrange("(g p t) i -> g p t i", g=2, t=4)
+
+        def load_y(g, h):
+            nc.sync.dma_start(out=y_sb[g, h][:], in_=y_rows[g][:, :, halves[h]])
 
         nc.sync.dma_start(out=x_win[0][:], in_=x_rows[0])
         nc.sync.dma_start(offsets[:], offs)
@@ -54,15 +56,15 @@ def tile_attend_gml_pl_nce_kernel(tc, xT, wd, wv, y, cw, rw, offs, out_0, out_1,
         nc.scalar.dma_start(out=rw_sb[:], in_=rw[0:1, :].rearrange("o (p c) -> (o p) c", c=4))
         for t in range(1, 4):
             nc.sync.dma_start(out=x_win[t][:], in_=x_rows[t])
-        for g in range(2):
-            nc.sync.dma_start(out=wd_raw[g][:], in_=wd_rows[:, :, 512 * g : 512 * (g + 1)])
-        for lanes in (slice(t, t + 1) for t in range(4)):
-            nc.sync.dma_start(out=y0[:, lanes, :], in_=y_rows[0][:, lanes, :])
-        nc.sync.dma_start(out=y1[0][:], in_=y_rows[1][:, :, : N // 2])
-        nc.sync.dma_start(out=wv_raw[0][:], in_=wv_rows[0])
         for h in range(2):
-            nc.sync.dma_start(out=wv_raw[1][h][:], in_=wv_rows[1][:, :, 256 * h : 256 * (h + 1)])
-        nc.sync.dma_start(out=y1[1][:], in_=y_rows[1][:, :, N // 2 :])
+            nc.sync.dma_start(out=wd_raw[0][h][:], in_=wd_rows[:, :, 256 * h : 256 * (h + 1)])
+        load_y(0, A)
+        nc.sync.dma_start(out=wd_raw[1][0][:], in_=wd_rows[:, :, 512:])
+        load_y(0, B)
+        nc.sync.dma_start(out=wv_raw[0][0][:], in_=wv_rows[0])
+        load_y(1, A)
+        nc.sync.dma_start(out=wv_raw[1][0][:], in_=wv_rows[1])
+        load_y(1, B)
 
         warm = new([P, 8], F32, "warm")
         nc.vector.memset(warm[:, 0:1], 0.0)
@@ -70,9 +72,6 @@ def tile_attend_gml_pl_nce_kernel(tc, xT, wd, wv, y, cw, rw, offs, out_0, out_1,
         o_win = [new([P, T], F32, "o_win%d" % t) for t in range(4)]
         for t in range(2):
             nc.vector.memset(o_win[t][:].bitcast(I32), 0)
-        g1_codes, g1_scales = new([P, N], U32, "g1_codes"), new([P, N], U8, "g1_scales")
-        nc.vector.memset(g1_codes[:, N // 2 :], 0)
-        nc.vector.memset(g1_scales[:, N // 2 :].bitcast(U32), 0)
         ident = new([P, P], F32, "ident")
         make_identity(nc, ident[:])
         for t in range(2, 4):
@@ -81,225 +80,197 @@ def tile_attend_gml_pl_nce_kernel(tc, xT, wd, wv, y, cw, rw, offs, out_0, out_1,
         for c in range(4):
             nc.tensor.transpose(rw_bank[:, c, :], rw_sb[:, c : c + 1].to_broadcast([P, P]), ident[:])
         rw_all = rw_bank[:].rearrange("p c n -> p n c")
-        w_cols = [(0, slice(0, 32)), (0, slice(32, 128)), (1, slice(0, 64)), (1, slice(64, 64 + OWN // 4)), (1, slice(64 + OWN // 4, 128))]
-        w_sb = [new([P, quads.stop - quads.start, 4, 4], F32, "w_sb%d" % k) for k, (g, quads) in enumerate(w_cols)]
-        for k, (g, quads) in enumerate(w_cols):
+        w_sb = [new([P, N // 4, 4, 4], F32, "w_sb%d" % g) for g in range(2)]
+        for g in range(2):
             for t in range(4):
-                nc.scalar.activation(w_sb[k][:, :, t, :], rw_all[:, quads, :], ACT.Copy, scale=cw_sb[:, g, t : t + 1])
+                nc.scalar.activation(w_sb[g][:, :, t, :], rw_all, ACT.Copy, scale=cw_sb[:, g, t : t + 1])
 
-        def quantize(grouped, width, fmt, name, tag=None):
-            codes = new([P, width], U32, name + "_codes", tag)
-            scales = new([P, width], U8, name + "_scales")
-            nc.vector.quantize_mx(out=codes[:].bitcast(fmt), scales=scales[:], in_=grouped)
-            return codes, scales
+        def operand(width, name, tag=None):
+            return new([P, width], U32, name + "_codes", tag), new([P, width], U8, name + "_scales")
+
+        def quantize(dst, cols, grouped, fmt):
+            nc.vector.quantize_mx(out=dst[0][:, cols].bitcast(fmt), scales=dst[1][:, cols], in_=grouped)
 
         x_g = new([P, N, 4], BF16, "x_g")
         for t in range(3):
             nc.vector.tensor_copy(x_g[:, :, t], x_win[t][:].indirect(offsets[:]))
         for h in range(2):
-            nc.vector.tensor_copy(x_g[:, 256 * h : 256 * (h + 1), 3], x_win[3][:].indirect(offsets[:, 16 * h : 16 * (h + 1)]))
-        x_q = (new([P, N], U32, "x_codes"), new([P, N], U8, "x_scales"))
+            nc.vector.tensor_copy(x_g[:, halves[h], 3], x_win[3][:].indirect(offsets[:, half_offsets[h]]))
+        x_q = [operand(HALF, "x%d" % h) for h in range(2)]
         for h in range(2):
-            cols = slice(256 * h, 256 * (h + 1))
-            nc.vector.quantize_mx(out=x_q[0][:, cols].bitcast(E4M3), scales=x_q[1][:, cols], in_=x_g[:, cols].rearrange("p n t -> p (n t)"))
+            quantize(x_q[h], slice(0, HALF), x_g[:, halves[h]].rearrange("p n t -> p (n t)"), E4M3)
 
-        def deal(raw, h, name, on_vector, tag=None, dealt=None):
-            if dealt is None:
-                dealt = new([P, 2, P, 4], BF16, name, tag)
-            pieces = raw if isinstance(raw, list) else [raw]
-            for k, piece in enumerate(pieces):
-                src = piece[:].rearrange("p j (m t) -> p m j t", t=4)[:, :, :, 2 * h : 2 * h + 2]
-                dst = dealt[:].rearrange("p t m j -> p m j t")[:, P // len(pieces) * k : P // len(pieces) * (k + 1)]
-                if on_vector:
-                    nc.vector.tensor_copy(dst, src)
-                else:
-                    nc.scalar.copy(dst, src)
-            return dealt
+        def deal(dealt, raw, k, piece, copy):
+            rows = P // len(raw)
+            src = raw[piece][:].rearrange("p j (m t) -> p m j t", t=4)[:, :, :, 2 * k : 2 * k + 2]
+            copy(dealt[:].rearrange("p t m j -> p m j t")[:, rows * piece : rows * (piece + 1)], src)
 
-        def quantize_half(dealt, name, tag=None):
-            return quantize(dealt[:].rearrange("p t m j -> p (t m j)"), 2 * P, E4M3, name, tag)
+        def dealt_tile(name, tag=None):
+            return new([P, 2, P, 4], BF16, name, tag)
 
-        def stationary(halves, t):
-            codes, scales = halves[t // 2]
-            cols = slice(P * (t % 2), P * (t % 2 + 1))
-            return codes[:, cols].bitcast(E4M3), scales[:, cols]
+        def quantize_pair(dealt, name):
+            q = operand(2 * P, name)
+            quantize(q, slice(0, 2 * P), dealt[:].rearrange("p t m j -> p (t m j)"), E4M3)
+            return q
 
-        s_lanes = [[slice(t, t + 1) for t in range(4)], [slice(0, 2), slice(2, 4)]]
-        s1 = new([P, 4, N // 2], F32, "s1")
-        s_sb = [[new([P, 1, N], F32, "s_sb0%d" % t) for t in range(4)], [s1[:, :2], s1[:, 2:]]]
-        halves = [slice(0, N // 2), slice(N // 2, N)]
-        parts = [slice(0, P), slice(P, N)]
+        def mx(out, lhs, e, rhs, cols, fmt, start, stop):
+            lane = slice(P * e, P * (e + 1))
+            nc.tensor.matmul_mx(out=out, lhsT=lhs[0][:, lane].bitcast(E4M3), lhsT_scale=lhs[1][:, lane], rhs=rhs[0][:, cols].bitcast(fmt), rhs_scale=rhs[1][:, cols], start=start, stop=stop)
 
-        def scores(g, wd_q):
-            banks = []
-            for k, lanes in enumerate(s_lanes[g]):
-                for t in range(lanes.start, lanes.stop):
-                    bank = psum.tile([P, N], F32, name="bank")
-                    lhs, lhs_s = stationary(wd_q, t)
-                    nc.tensor.matmul_mx(out=bank[:], lhsT=lhs, lhsT_scale=lhs_s, rhs=x_q[0][:].bitcast(E4M3), rhs_scale=x_q[1][:], start=True, stop=True)
-                    banks.append(bank)
-                    for cols in [halves[0]] if g else parts if t == 3 else [slice(0, N)]:
-                        nc.scalar.activation(s_sb[g][k][:, t - lanes.start, cols], bank[:, cols], ACT.Sigmoid)
-            return banks
+        s_sb = {(g, h): new([P, 4, HALF], F32, "s%d%d" % (g, h)) for g in range(2) for h in range(2)}
+        grad = {(g, h): new([P, HALF, 4], BF16, "grad%d%d" % (g, h)) for g in range(2) for h in range(2)}
+        g_q = [operand(N, "g%d" % g) for g in range(2)]
 
-        def subtract0(k):
-            lanes = s_lanes[0][k]
-            for cols in parts if k == 3 else [slice(0, N)]:
-                nc.vector.tensor_tensor(y0[:, lanes, cols], s_sb[0][k][:, :, cols], y0[:, lanes, cols], ALU.subtract)
+        def scores(wd_q, g, h, k):
+            bank = psum.tile([P, 2, HALF], F32, name="bank")
+            for e in range(2):
+                mx(bank[:, e], wd_q[k], e, x_q[h], slice(0, HALF), E4M3, True, True)
+            nc.scalar.activation(s_sb[g, h][:, 2 * k : 2 * k + 2], bank[:], ACT.Sigmoid)
 
-        def subtract1(h, s_half, lanes, cols, out=None):
-            y_part = y1[h][:, lanes, cols]
-            nc.vector.tensor_tensor(y_part if out is None else out, s_half[:, lanes, cols], y_part, ALU.subtract)
+        def subtract(g, h, lanes):
+            nc.vector.tensor_tensor(y_sb[g, h][:, lanes], s_sb[g, h][:, lanes], y_sb[g, h][:, lanes], ALU.subtract)
 
-        def weigh(k, diff, grad, engine=nc.vector):
-            engine.tensor_tensor(
-                grad.rearrange("p (c i) t -> p c t i", i=4),
-                diff.rearrange("p t (c i) -> p c t i", i=4),
-                w_sb[k][:],
+        def weigh(g, h):
+            nc.vector.tensor_tensor(
+                grad[g, h][:].rearrange("p (c i) t -> p c t i", i=4),
+                y_sb[g, h][:].rearrange("p t (c i) -> p c t i", i=4),
+                w_sb[g][:, 64 * h : 64 * (h + 1)],
                 ALU.mult,
             )
 
-        wd00 = deal(wd_raw[0], 0, "wd00", True)
-        wd01 = deal(wd_raw[0], 1, "wd01", False)
-        wd00_q = (new([P, 2 * P], U32, "wd00_codes"), new([P, 2 * P], U8, "wd00_scales"))
-        for t in range(2):
-            cols = slice(P * t, P * (t + 1))
-            nc.vector.quantize_mx(out=wd00_q[0][:, cols].bitcast(E4M3), scales=wd00_q[1][:, cols], in_=wd00[:, t].rearrange("p m j -> p (m j)"))
-        wd0_q = [wd00_q, quantize_half(wd01, "wd01")]
-        scores(0, wd0_q)
-        wd10 = deal(wd_raw[1], 0, "wd10", True)
-        subtract0(0)
-        wd1_q = [quantize_half(wd10, "wd10")]
-        wd11 = deal(wd_raw[1], 1, "wd11", False, "wd01_codes")
-        for k in (1, 2, 3):
-            subtract0(k)
-        grad0 = new([P, N, 4], BF16, "grad0")
-        weigh(0, y0[:, :, parts[0]], grad0[:, parts[0]])
-        wd1_q.append(quantize_half(wd11, "wd11", "s_sb03"))
-        weigh(1, y0[:, :, parts[1]], grad0[:, parts[1]])
-        banks1 = {}
+        def quantize_g(g, h):
+            quantize(g_q[g], halves[h], grad[g, h][:].rearrange("p n t -> p (n t)"), E5M2)
+
+        low, high = slice(0, 2), slice(2, 4)
+
+        wd0 = [dealt_tile("wd0%d" % k) for k in range(2)]
+        deal(wd0[0], wd_raw[0], 0, 0, nc.scalar.copy)
+        deal(wd0[1], wd_raw[0], 1, 0, nc.scalar.copy)
+        deal(wd0[0], wd_raw[0], 0, 1, nc.vector.tensor_copy)
+        deal(wd0[1], wd_raw[0], 1, 1, nc.scalar.copy)
+        wd0_q = [operand(2 * P, "wd00")]
+        for e in range(2):
+            quantize(wd0_q[0], slice(P * e, P * (e + 1)), wd0[0][:, e].rearrange("p m j -> p (m j)"), E4M3)
+        wd0_q.append(quantize_pair(wd0[1], "wd01"))
+        for h in range(2):
+            for k in range(2):
+                scores(wd0_q, 0, h, k)
+        subtract(0, A, low)
+        subtract(0, A, high)
+        wd1 = [dealt_tile("wd1%d" % k) for k in range(2)]
         for k in range(2):
-            for h in range(2):
-                banks1[k, h] = psum.tile([P, 2, N // 2], F32, name="bank")
-                for e in range(2):
-                    lhs, lhs_s = stationary(wd1_q, 2 * k + e)
-                    nc.tensor.matmul_mx(out=banks1[k, h][:, e], lhsT=lhs, lhsT_scale=lhs_s, rhs=x_q[0][:, halves[h]].bitcast(E4M3), rhs_scale=x_q[1][:, halves[h]], start=True, stop=True)
-            nc.scalar.activation(s1[:, 2 * k : 2 * k + 2], banks1[k, 0][:], ACT.Sigmoid)
+            deal(wd1[k], wd_raw[1], k, 0, nc.scalar.copy)
+        weigh(0, A)
+        subtract(0, B, slice(0, 4))
+        wd1_q = [quantize_pair(wd1[0], "wd10")]
+        weigh(0, B)
+        wd1_q.append(quantize_pair(wd1[1], "wd11"))
+        quantize_g(0, A)
+        quantize_g(0, B)
 
-        wv0a = deal(wv_raw[0], 1, "wv0a", False, "x_codes")
-        wv1a = deal(wv_raw[1], 1, "wv1a", False)
-        s1b = new([P, 4, N // 2], F32, "s1b")
-        for k in range(2):
-            nc.scalar.activation(s1b[:, 2 * k : 2 * k + 2], banks1[k, 1][:], ACT.Sigmoid)
-        mine, pools = slice(0, OWN), slice(OWN, N // 2)
-        subtract1(0, s1, slice(0, 2), halves[0])
-        subtract1(0, s1, slice(2, 4), halves[0])
-        g0_codes, g0_scales = quantize(grad0[:].rearrange("p n t -> p (n t)"), N, E5M2, "g0")
-        grad1 = new([P, N // 2, 4], BF16, "grad1")
-        weigh(2, y1[0][:], grad1[:])
-        wv0a_q = quantize_half(wv0a, "wv0a", "grad0")
-
-        def quantize_g1(grad, first):
-            cols = slice(first, first + grad.shape[1])
-            nc.vector.quantize_mx(out=g1_codes[:, cols].bitcast(E5M2), scales=g1_scales[:, cols], in_=grad.rearrange("p n t -> p (n t)"))
-
-        quantize_g1(grad1[:], 0)
-        wv1a_q = quantize_half(wv1a, "wv1a")
+        wv = {}
         wv_q = {}
-        for t in (2, 3):
-            wv_q[t, 0] = wv0a_q + (P * (t - 2),)
-            wv_q[t, 1] = wv1a_q + (P * (t - 2),)
-        g_q = [(g0_codes, g0_scales), (g1_codes, g1_scales)]
+        scores(wd1_q, 1, A, 0)
+        wv[0, 1] = dealt_tile("wv01")
+        scores(wd1_q, 1, A, 1)
+        deal(wv[0, 1], wv_raw[0], 1, 0, nc.scalar.copy)
+        wv[1, 1] = dealt_tile("wv11")
+        deal(wv[1, 1], wv_raw[1], 1, 0, nc.scalar.copy)
+        for k in range(2):
+            scores(wd1_q, 1, B, k)
+        subtract(1, A, low)
+        subtract(1, A, high)
+        wv_q[0, 1] = quantize_pair(wv[0, 1], "wv01")
+        weigh(1, A)
+        wv[0, 0] = dealt_tile("wv00")
+        deal(wv[0, 0], wv_raw[0], 0, 0, nc.vector.tensor_copy)
+        quantize_g(1, A)
+        wv_q[1, 1] = quantize_pair(wv[1, 1], "wv11")
+        wv[1, 0] = dealt_tile("wv10")
+        deal(wv[1, 0], wv_raw[1], 0, 0, nc.scalar.copy)
+        subtract(1, B, slice(0, 4))
+        weigh(1, B)
 
-        def product(t, passes=(0, 1)):
-            bank = psum.tile([P, N], F32, name="bank")
-            for g in passes:
-                codes, scales, first = wv_q[t, g]
-                lhs, lhs_s = codes[:, first : first + P].bitcast(E4M3), scales[:, first : first + P]
-                nc.tensor.matmul_mx(out=bank[:], lhsT=lhs, lhsT_scale=lhs_s, rhs=g_q[g][0][:].bitcast(E5M2), rhs_scale=g_q[g][1][:], start=(g == passes[0]), stop=(g == passes[1]))
+        def product(t, cols):
+            bank = psum.tile([P, cols.stop - cols.start], F32, name="bank")
+            for g in range(2):
+                mx(bank[:], wv_q[g, t // 2], t % 2, g_q[g], cols, E5M2, g == 0, g == 1)
             return bank
 
-        early = {2: product(2), 3: product(3, (1, 0))}
-        diff = new([P, 4, N // 2], F32, "diff", "wv1a")
-        subtract1(1, s1b, slice(0, 4), halves[0], diff[:])
-        grad_pool = new([P, N // 2 - OWN, 4], BF16, "grad_pool")
-        weigh(4, diff[:, :, pools], grad_pool[:], nc.gpsimd)
-        dx_a = {2: new([P, N // 2], F32, "dx_a2")}
-        nc.scalar.copy(dx_a[2][:], early[2][:, halves[0]])
-        wv0b = deal(wv_raw[0], 0, "wv0b", False, "y11")
-        nc.vector.tensor_copy(o_win[2][:].indirect(offsets[:, :16]), dx_a[2][:])
-        grad_mine = new([P, OWN, 4], BF16, "grad_mine", "w_sb4")
-        weigh(3, diff[:, :, mine], grad_mine[:])
-        dx_a[3] = new([P, N // 2], F32, "dx_a3", "w_sb3")
-        nc.scalar.copy(dx_a[3][:], early[3][:, halves[0]])
-        wv1b = deal(wv_raw[1], 0, "wv1b", False, "wv1a")
-        quantize_g1(grad_pool[:], N // 2 + OWN)
-        wv_b_q = [quantize_half(wv0b, "wv0b")]
-        quantize_g1(grad_mine[:], N // 2)
-        nc.vector.tensor_copy(o_win[3][:].indirect(offsets[:, :16]), dx_a[3][:])
-        wv_b_q.append(quantize_half(wv1b, "wv1b"))
-        for g in range(2):
-            for t in (0, 1):
-                wv_q[t, g] = wv_b_q[g] + (P * t,)
-        stage = new([P, N + 256 * 2 * (8 - DIRECT)], F32, "stage", "wv1b_codes")
-        dx = {2: new([P, N // 2], F32, "dx2", "wv_raw11")[:], 0: new([P, N], F32, "dx0")[:], 3: new([P, N // 2], F32, "dx3")[:], 1: stage[:, :N]}
-        for t in (2, 3, 0, 1):
-            nc.scalar.copy(dx[t], product(t, (1, 0) if t >= 2 else (0, 1))[:, halves[1] if t >= 2 else slice(0, N)])
-
         out_rows = out_0.rearrange("(p t) c -> t p c", t=4)
-        pairs = stage[:, N:].bitcast(BF16).rearrange("p (k u c e) -> p k u c e", k=8 - DIRECT, u=2, e=2)
-        chunks = len(GROUPS)
-        reuse = [None, "x_win1", "x_win2", "x_win3", "x_win0"]
-        woven = [new([P, hi - lo, 256, 2, 2], BF16, "woven%d" % k, tag=reuse[k]) for k, (lo, hi) in enumerate(GROUPS)]
-        direct = woven[0][:].rearrange("p k c u e -> p (k c) (u e)")
-        one = direct[:, 0, 1:2]
-        nc.gpsimd.memset(one, 1.0)
+        GROUPS = [(0, 1024), (1024, 1536), (1536, 2048)]
+        pairs = [new([P, 2, hi - lo, 2], BF16, "pairs%d" % k) for k, (lo, hi) in enumerate(GROUPS)]
+        dx = {(t, h): new([P, HALF], F32, "dx%d%d" % (t, h))[:] for t in range(4) for h in range(2) if (t, h) != (1, A)}
+        dx[1, A] = pairs[2][:, 1, :HALF].rearrange("p c e -> p (c e)").bitcast(F32)
 
-        def strips(t, lo, hi):
-            return pairs[:, lo - DIRECT : hi - DIRECT, t // 2, :, t % 2], o_win[t][:, 256 * lo : 256 * hi].rearrange("p (k c) -> p k c", c=256)
+        def scatter_early(t):
+            nc.scalar.activation(o_win[t][:].indirect(offsets[:, half_offsets[A]]), dx[t, A], ACT.Copy)
 
-        def weave(lo, hi, k):
-            first = GROUPS[k][0]
-            dst = woven[k][:, lo - first : hi - first].rearrange("p k c u e -> p k c (u e)")
-            src = pairs[:, lo - DIRECT : hi - DIRECT].rearrange("p k u c e -> p k u (c e)")
-            if lo < WEAVE_SPLIT:
-                nc.vector.tensor_copy(dst.bitcast(I32), src.bitcast(I32).rearrange("p k u c -> p k c u"))
-            else:
-                nc.scalar.copy(dst.bitcast(U32), src.bitcast(U32).rearrange("p k u c -> p k c u"))
-
-        for t in (2, 3, 0, 1):
-            nc.vector.tensor_copy(o_win[t][:].indirect(offsets[:, 16:] if t >= 2 else offsets[:]), dx[t])
+        def scatter_late(t):
+            nc.vector.tensor_copy(o_win[t][:].indirect(offsets[:, half_offsets[B]]), dx[t, B])
             nc.sync.dma_start(out=out_rows[t], in_=o_win[t][:])
-            if t == 1:
-                break
-            nc.scalar.copy(*strips(t, DIRECT, POOL_STRIP if t else 8))
-            if t:
-                nc.gpsimd.tensor_scalar(*strips(t, POOL_STRIP, 8), 1.0, -0.0, ALU.mult, ALU.add)
-            nc.gpsimd.tensor_scalar(direct[:, :, t], o_win[t][:, : 256 * DIRECT], 1.0 if t else one, -0.0, ALU.mult, ALU.add)
 
-        nc.vector.tensor_copy(direct[:, :, 1], o_win[1][:, : 256 * DIRECT])
-        nc.scalar.copy(*strips(1, 2, 4))
-        nc.scalar.copy(*strips(1, 4, 6))
-        nc.scalar.copy(*strips(1, 6, 7))
-        weave(5, 6, 2)
-        nc.scalar.copy(*strips(1, 7, 8))
-        weave(6, 7, 3)
-        weave(7, 8, 4)
+        def rounded(t, k, lo, hi):
+            first = GROUPS[k][0]
+            return pairs[k][:, t // 2, lo - first : hi - first, t % 2], o_win[t][:, lo:hi]
 
+        for t in (2, 3):
+            nc.scalar.copy(dx[t, A], product(t, halves[A])[:])
+            scatter_early(t)
+        wv_q[0, 0] = quantize_pair(wv[0, 0], "wv00")
+        quantize_g(1, B)
+        late = {t: product(t, halves[B]) for t in (2, 3)}
+        wv_q[1, 0] = quantize_pair(wv[1, 0], "wv10")
+        for t in (0, 1):
+            nc.scalar.copy(dx[t, A], product(t, halves[A])[:])
+        for t in (0, 1):
+            scatter_early(t)
+            late[t] = product(t, halves[B])
+        for t in (2, 3):
+            nc.vector.tensor_copy(dx[t, B], late[t][:])
+        scatter_late(2)
+        for t in (0, 1):
+            nc.vector.tensor_copy(dx[t, B], late[t][:])
+        for t in (3, 0, 1):
+            scatter_late(t)
+        for t in (2, 3):
+            for k in range(2):
+                nc.gpsimd.tensor_scalar(*rounded(t, k, *GROUPS[k]), 1.0, -0.0, ALU.mult, ALU.add)
+        for t in (2, 3):
+            nc.scalar.copy(*rounded(t, 2, *GROUPS[2]))
+
+        CHUNKS = [(0, 0, 512), (0, 512, 1024), (1, 1024, 1536), (2, 1536, 1792), (2, 1792, 2048)]
+        reuse = ["x_win0", "x_win1", "x_win2", "x_win3", "wd_raw1"]
+        woven = [new([P, hi - lo, 2, 2], BF16, "woven%d" % c, tag=reuse[c]) for c, (k, lo, hi) in enumerate(CHUNKS)]
         words_out = out_1.rearrange("o p c l -> p (o c l)").bitcast(I32)
         o_scales = new([P, T // 2], U8, "o_scales")
-        o_codes = [new([P, 256 * (hi - lo)], U32, "o_codes%d" % k) for k, (lo, hi) in enumerate(GROUPS)]
+        o_codes = [new([P, hi - lo], U32, "o_codes%d" % c) for c, (k, lo, hi) in enumerate(CHUNKS)]
 
-        def emit(k):
-            cols = slice(256 * GROUPS[k][0], 256 * GROUPS[k][1])
-            nc.vector.quantize_mx(out=o_codes[k][:].bitcast(E4M3), scales=o_scales[4 * (cols.start // 1024) :, cols.start % 1024 : cols.start % 1024 + cols.stop - cols.start], in_=woven[k][:].rearrange("p k c u e -> p (k c u e)"))
-            nc.sync.dma_start(out=words_out[:, cols], in_=o_codes[k][:].bitcast(I32))
+        def weave(c, copy, word):
+            k, lo, hi = CHUNKS[c]
+            first = GROUPS[k][0]
+            src = pairs[k][:, :, lo - first : hi - first].rearrange("p u c e -> p u (c e)").bitcast(word)
+            copy(woven[c][:].rearrange("p c u e -> p c (u e)").bitcast(word), src.rearrange("p u c -> p c u"))
 
-        weave(2, 4, 1)
-        emit(0)
-        weave(4, 5, 2)
-        for k in range(1, chunks):
-            emit(k)
+        def emit(c):
+            k, lo, hi = CHUNKS[c]
+            nc.vector.quantize_mx(out=o_codes[c][:].bitcast(E4M3), scales=o_scales[4 * (lo // 1024) :, lo % 1024 : lo % 1024 + hi - lo], in_=woven[c][:].rearrange("p c u e -> p (c u e)"))
+            nc.sync.dma_start(out=words_out[:, lo:hi], in_=o_codes[c][:].bitcast(I32))
+
+        nc.scalar.copy(*rounded(0, 1, *GROUPS[1]))
+        nc.scalar.copy(*rounded(0, 2, *GROUPS[2]))
+        nc.scalar.copy(*rounded(1, 1, *GROUPS[1]))
+        nc.scalar.copy(*rounded(1, 2, *GROUPS[2]))
+        weave(2, nc.scalar.copy, U32)
+        weave(3, nc.scalar.copy, U32)
+        weave(4, nc.scalar.copy, U32)
+        nc.vector.tensor_copy(*rounded(0, 0, 0, 1024))
+        nc.vector.tensor_copy(*rounded(1, 0, 0, 512))
+        nc.vector.tensor_copy(*rounded(1, 0, 512, 1024))
+        weave(0, nc.vector.tensor_copy, I32)
+        weave(1, nc.vector.tensor_copy, I32)
+        for c in range(len(CHUNKS)):
+            emit(c)
         scales_out = out_2.rearrange("o f c -> (o f) c").bitcast(I32).rearrange("f (h c) -> h f c", h=2)
         for q in range(4):
             nc.sync.dma_start(out=scales_out[:, 4 * q : 4 * q + 4, :], in_=o_scales[32 * q : 32 * q + 8, :].bitcast(I32))

@@ -64,7 +64,8 @@ def tile_attend_gml_pl_nce_kernel(tc, xT, wd, wv, y, cw, rw, offs, out_0, out_1,
         nc.sync.dma_start(out=wv_raw[0][0][:], in_=wv_rows[0])
         load_y(1, A)
         nc.sync.dma_start(out=wv_raw[1][0][:], in_=wv_rows[1])
-        load_y(1, B)
+        for lanes in (slice(0, 2), slice(2, 4)):
+            nc.sync.dma_start(out=y_sb[1, B][:, lanes], in_=y_rows[1][:, lanes, halves[B]])
 
         warm = new([P, 8], F32, "warm")
         nc.vector.memset(warm[:, 0:1], 0.0)
@@ -118,28 +119,30 @@ def tile_attend_gml_pl_nce_kernel(tc, xT, wd, wv, y, cw, rw, offs, out_0, out_1,
             nc.tensor.matmul_mx(out=out, lhsT=lhs[0][:, lane].bitcast(E4M3), lhsT_scale=lhs[1][:, lane], rhs=rhs[0][:, cols].bitcast(fmt), rhs_scale=rhs[1][:, cols], start=start, stop=stop)
 
         s_sb = {(g, h): new([P, 4, HALF], F32, "s%d%d" % (g, h)) for g in range(2) for h in range(2)}
-        grad = {(g, h): new([P, HALF, 4], BF16, "grad%d%d" % (g, h)) for g in range(2) for h in range(2)}
+        grad0 = new([P, N, 4], BF16, "grad0")
+        grad = {(0, h): grad0[:, halves[h]] for h in range(2)}
+        grad.update({(1, h): new([P, HALF, 4], BF16, "grad1%d" % h)[:] for h in range(2)})
         g_q = [operand(N, "g%d" % g) for g in range(2)]
 
-        def scores(wd_q, g, h, k):
-            bank = psum.tile([P, 2, HALF], F32, name="bank")
-            for e in range(2):
-                mx(bank[:, e], wd_q[k], e, x_q[h], slice(0, HALF), E4M3, True, True)
-            nc.scalar.activation(s_sb[g, h][:, 2 * k : 2 * k + 2], bank[:], ACT.Sigmoid)
+        def scores(wd_q, g, h, lanes):
+            bank = psum.tile([P, lanes.stop - lanes.start, HALF], F32, name="bank")
+            for t in range(lanes.start, lanes.stop):
+                mx(bank[:, t - lanes.start], wd_q[t // 2], t % 2, x_q[h], slice(0, HALF), E4M3, True, True)
+            nc.scalar.activation(s_sb[g, h][:, lanes], bank[:], ACT.Sigmoid)
 
         def subtract(g, h, lanes):
             nc.vector.tensor_tensor(y_sb[g, h][:, lanes], s_sb[g, h][:, lanes], y_sb[g, h][:, lanes], ALU.subtract)
 
-        def weigh(g, h):
+        def weigh(g, h, lo=0, hi=HALF):
             nc.vector.tensor_tensor(
-                grad[g, h][:].rearrange("p (c i) t -> p c t i", i=4),
-                y_sb[g, h][:].rearrange("p t (c i) -> p c t i", i=4),
-                w_sb[g][:, 64 * h : 64 * (h + 1)],
+                grad[g, h][:, lo:hi].rearrange("p (c i) t -> p c t i", i=4),
+                y_sb[g, h][:, :, lo:hi].rearrange("p t (c i) -> p c t i", i=4),
+                w_sb[g][:, (HALF * h + lo) // 4 : (HALF * h + hi) // 4],
                 ALU.mult,
             )
 
-        def quantize_g(g, h):
-            quantize(g_q[g], halves[h], grad[g, h][:].rearrange("p n t -> p (n t)"), E5M2)
+        def quantize_g(g, h, lo=0, hi=HALF):
+            quantize(g_q[g], slice(HALF * h + lo, HALF * h + hi), grad[g, h][:, lo:hi].rearrange("p n t -> p (n t)"), E5M2)
 
         low, high = slice(0, 2), slice(2, 4)
 
@@ -152,11 +155,13 @@ def tile_attend_gml_pl_nce_kernel(tc, xT, wd, wv, y, cw, rw, offs, out_0, out_1,
         for e in range(2):
             quantize(wd0_q[0], slice(P * e, P * (e + 1)), wd0[0][:, e].rearrange("p m j -> p (m j)"), E4M3)
         wd0_q.append(quantize_pair(wd0[1], "wd01"))
-        for h in range(2):
-            for k in range(2):
-                scores(wd0_q, 0, h, k)
-        subtract(0, A, low)
-        subtract(0, A, high)
+        single = [slice(t, t + 1) for t in range(4)]
+        for lanes in single:
+            scores(wd0_q, 0, A, lanes)
+        for lanes in (low, high):
+            scores(wd0_q, 0, B, lanes)
+        for lanes in single:
+            subtract(0, A, lanes)
         wd1 = [dealt_tile("wd1%d" % k) for k in range(2)]
         for k in range(2):
             deal(wd1[k], wd_raw[1], k, 0, nc.scalar.copy)
@@ -165,31 +170,29 @@ def tile_attend_gml_pl_nce_kernel(tc, xT, wd, wv, y, cw, rw, offs, out_0, out_1,
         wd1_q = [quantize_pair(wd1[0], "wd10")]
         weigh(0, B)
         wd1_q.append(quantize_pair(wd1[1], "wd11"))
-        quantize_g(0, A)
-        quantize_g(0, B)
+        quantize(g_q[0], slice(0, N), grad0[:].rearrange("p n t -> p (n t)"), E5M2)
 
-        wv = {}
+        wv_d = {(g, k): dealt_tile("wv%d%d" % (g, k)) for g in range(2) for k in range(2)}
         wv_q = {}
-        scores(wd1_q, 1, A, 0)
-        wv[0, 1] = dealt_tile("wv01")
-        scores(wd1_q, 1, A, 1)
-        deal(wv[0, 1], wv_raw[0], 1, 0, nc.scalar.copy)
-        wv[1, 1] = dealt_tile("wv11")
-        deal(wv[1, 1], wv_raw[1], 1, 0, nc.scalar.copy)
-        for k in range(2):
-            scores(wd1_q, 1, B, k)
+        scores(wd1_q, 1, A, low)
+        scores(wd1_q, 1, A, high)
+        deal(wv_d[0, 1], wv_raw[0], 1, 0, nc.scalar.copy)
+        deal(wv_d[1, 1], wv_raw[1], 1, 0, nc.scalar.copy)
+        for lanes in (low, high):
+            scores(wd1_q, 1, B, lanes)
+        deal(wv_d[1, 0], wv_raw[1], 0, 0, nc.scalar.copy)
         subtract(1, A, low)
         subtract(1, A, high)
-        wv_q[0, 1] = quantize_pair(wv[0, 1], "wv01")
+        deal(wv_d[0, 0], wv_raw[0], 0, 0, nc.vector.tensor_copy)
+        wv_q[0, 1] = quantize_pair(wv_d[0, 1], "wv01")
         weigh(1, A)
-        wv[0, 0] = dealt_tile("wv00")
-        deal(wv[0, 0], wv_raw[0], 0, 0, nc.vector.tensor_copy)
+        subtract(1, B, low)
+        wv_q[1, 1] = quantize_pair(wv_d[1, 1], "wv11")
         quantize_g(1, A)
-        wv_q[1, 1] = quantize_pair(wv[1, 1], "wv11")
-        wv[1, 0] = dealt_tile("wv10")
-        deal(wv[1, 0], wv_raw[1], 0, 0, nc.scalar.copy)
-        subtract(1, B, slice(0, 4))
-        weigh(1, B)
+        subtract(1, B, high)
+        wv_q[0, 0] = quantize_pair(wv_d[0, 0], "wv00")
+        weigh(1, B, 0, P)
+        weigh(1, B, P, HALF)
 
         def product(t, cols):
             bank = psum.tile([P, cols.stop - cols.start], F32, name="bank")
@@ -208,6 +211,8 @@ def tile_attend_gml_pl_nce_kernel(tc, xT, wd, wv, y, cw, rw, offs, out_0, out_1,
 
         def scatter_late(t):
             nc.vector.tensor_copy(o_win[t][:].indirect(offsets[:, half_offsets[B]]), dx[t, B])
+
+        def store(t):
             nc.sync.dma_start(out=out_rows[t], in_=o_win[t][:])
 
         def rounded(t, k, lo, hi):
@@ -217,10 +222,10 @@ def tile_attend_gml_pl_nce_kernel(tc, xT, wd, wv, y, cw, rw, offs, out_0, out_1,
         for t in (2, 3):
             nc.scalar.copy(dx[t, A], product(t, halves[A])[:])
             scatter_early(t)
-        wv_q[0, 0] = quantize_pair(wv[0, 0], "wv00")
-        quantize_g(1, B)
+        quantize_g(1, B, 0, P)
+        quantize_g(1, B, P, HALF)
         late = {t: product(t, halves[B]) for t in (2, 3)}
-        wv_q[1, 0] = quantize_pair(wv[1, 0], "wv10")
+        wv_q[1, 0] = quantize_pair(wv_d[1, 0], "wv10")
         for t in (0, 1):
             nc.scalar.copy(dx[t, A], product(t, halves[A])[:])
         for t in (0, 1):
@@ -229,10 +234,12 @@ def tile_attend_gml_pl_nce_kernel(tc, xT, wd, wv, y, cw, rw, offs, out_0, out_1,
         for t in (2, 3):
             nc.vector.tensor_copy(dx[t, B], late[t][:])
         scatter_late(2)
+        store(2)
         for t in (0, 1):
             nc.vector.tensor_copy(dx[t, B], late[t][:])
         for t in (3, 0, 1):
             scatter_late(t)
+            store(t)
         for t in (2, 3):
             for k in range(2):
                 nc.gpsimd.tensor_scalar(*rounded(t, k, *GROUPS[k]), 1.0, -0.0, ALU.mult, ALU.add)

@@ -201,10 +201,10 @@ def tile_attend_gml_pl_nce_kernel(tc, xT, wd, wv, y, cw, rw, offs, out_0, out_1,
             return bank
 
         out_rows = out_0.rearrange("(p t) c -> t p c", t=4)
-        GROUPS = [(0, 1024), (1024, 1536), (1536, 2048)]
+        GROUPS = [(0, 1280), (1280, 2048)]
         pairs = [new([P, 2, hi - lo, 2], BF16, "pairs%d" % k) for k, (lo, hi) in enumerate(GROUPS)]
         dx = {(t, h): new([P, HALF], F32, "dx%d%d" % (t, h))[:] for t in range(4) for h in range(2) if (t, h) != (1, A)}
-        dx[1, A] = pairs[2][:, 1, :HALF].rearrange("p c e -> p (c e)").bitcast(F32)
+        dx[1, A] = pairs[1][:, 1, :HALF].rearrange("p c e -> p (c e)").bitcast(F32)
 
         def scatter_early(t):
             nc.scalar.activation(o_win[t][:].indirect(offsets[:, half_offsets[A]]), dx[t, A], ACT.Copy)
@@ -241,12 +241,11 @@ def tile_attend_gml_pl_nce_kernel(tc, xT, wd, wv, y, cw, rw, offs, out_0, out_1,
             scatter_late(t)
             store(t)
         for t in (2, 3):
-            for k in range(2):
-                nc.gpsimd.tensor_scalar(*rounded(t, k, *GROUPS[k]), 1.0, -0.0, ALU.mult, ALU.add)
+            nc.gpsimd.tensor_scalar(*rounded(t, 0, *GROUPS[0]), 1.0, -0.0, ALU.mult, ALU.add)
         for t in (2, 3):
-            nc.scalar.copy(*rounded(t, 2, *GROUPS[2]))
+            nc.scalar.copy(*rounded(t, 1, *GROUPS[1]))
 
-        CHUNKS = [(0, 0, 512), (0, 512, 1024), (1, 1024, 1536), (2, 1536, 1792), (2, 1792, 2048)]
+        CHUNKS = [(0, 0, 512), (0, 512, 1024), (0, 1024, 1280), (1, 1280, 1792), (1, 1792, 2048)]
         reuse = ["x_win0", "x_win1", "x_win2", "x_win3", "wd_raw1"]
         woven = [new([P, hi - lo, 2, 2], BF16, "woven%d" % c, tag=reuse[c]) for c, (k, lo, hi) in enumerate(CHUNKS)]
         words_out = out_1.rearrange("o p c l -> p (o c l)").bitcast(I32)
@@ -265,17 +264,15 @@ def tile_attend_gml_pl_nce_kernel(tc, xT, wd, wv, y, cw, rw, offs, out_0, out_1,
             nc.sync.dma_start(out=words_out[:, lo:hi], in_=o_codes[c][:].bitcast(I32))
 
         nc.scalar.copy(*rounded(0, 1, *GROUPS[1]))
-        nc.scalar.copy(*rounded(0, 2, *GROUPS[2]))
-        nc.scalar.copy(*rounded(1, 1, *GROUPS[1]))
-        nc.scalar.copy(*rounded(1, 2, *GROUPS[2]))
-        weave(2, nc.scalar.copy, U32)
-        weave(3, nc.scalar.copy, U32)
-        weave(4, nc.scalar.copy, U32)
-        nc.vector.tensor_copy(*rounded(0, 0, 0, 1024))
+        for c in (3, 4):
+            nc.scalar.copy(*rounded(1, *CHUNKS[c]))
+        for c in (3, 4):
+            weave(c, nc.scalar.copy, U32)
+        nc.vector.tensor_copy(*rounded(0, 0, *GROUPS[0]))
         nc.vector.tensor_copy(*rounded(1, 0, 0, 512))
-        nc.vector.tensor_copy(*rounded(1, 0, 512, 1024))
-        weave(0, nc.vector.tensor_copy, I32)
-        weave(1, nc.vector.tensor_copy, I32)
+        nc.vector.tensor_copy(*rounded(1, 0, 512, 1280))
+        for c in range(3):
+            weave(c, nc.vector.tensor_copy, I32)
         for c in range(len(CHUNKS)):
             emit(c)
         scales_out = out_2.rearrange("o f c -> (o f) c").bitcast(I32).rearrange("f (h c) -> h f c", h=2)

@@ -201,10 +201,11 @@ def tile_attend_gml_pl_nce_kernel(tc, xT, wd, wv, y, cw, rw, offs, out_0, out_1,
             return bank
 
         out_rows = out_0.rearrange("(p t) c -> t p c", t=4)
-        GROUPS = [(0, 1280), (1280, 2048)]
-        pairs = [new([P, 2, hi - lo, 2], BF16, "pairs%d" % k) for k, (lo, hi) in enumerate(GROUPS)]
+        GROUPS = [(0, T)]
+        POOL, MINE = 1408, 1152
+        pairs = [new([P, 2, T, 2], BF16, "pairs")]
         dx = {(t, h): new([P, HALF], F32, "dx%d%d" % (t, h))[:] for t in range(4) for h in range(2) if (t, h) != (1, A)}
-        dx[1, A] = pairs[1][:, 1, :HALF].rearrange("p c e -> p (c e)").bitcast(F32)
+        dx[1, A] = pairs[0][:, 1, T - HALF :].rearrange("p c e -> p (c e)").bitcast(F32)
 
         def scatter_early(t):
             nc.scalar.activation(o_win[t][:].indirect(offsets[:, half_offsets[A]]), dx[t, A], ACT.Copy)
@@ -241,16 +242,16 @@ def tile_attend_gml_pl_nce_kernel(tc, xT, wd, wv, y, cw, rw, offs, out_0, out_1,
             scatter_late(t)
             store(t)
         for t in (2, 3):
-            nc.gpsimd.tensor_scalar(*rounded(t, 0, *GROUPS[0]), 1.0, -0.0, ALU.mult, ALU.add)
+            nc.gpsimd.tensor_scalar(*rounded(t, 0, 0, POOL), 1.0, -0.0, ALU.mult, ALU.add)
         for t in (2, 3):
-            nc.scalar.copy(*rounded(t, 1, *GROUPS[1]))
+            nc.scalar.copy(*rounded(t, 0, POOL, T))
 
-        CHUNKS = [(0, 0, 512), (0, 512, 1024), (0, 1024, 1280), (1, 1280, 1792), (1, 1792, 2048)]
-        reuse = ["x_win0", "x_win1", "x_win2", "x_win3", "wd_raw1"]
+        CHUNKS = [(0, 0, 512), (0, 512, 1024), (0, 1024, 1152), (0, 1152, 1664), (0, 1664, 1920), (0, 1920, 2048)]
+        reuse = ["x_win0", "x_win1", "x_win2", "x_win3", "wd_raw1", "wv_raw0"]
         woven = [new([P, hi - lo, 2, 2], BF16, "woven%d" % c, tag=reuse[c]) for c, (k, lo, hi) in enumerate(CHUNKS)]
         words_out = out_1.rearrange("o p c l -> p (o c l)").bitcast(I32)
         o_scales = new([P, T // 2], U8, "o_scales")
-        o_codes = [new([P, hi - lo], U32, "o_codes%d" % c) for c, (k, lo, hi) in enumerate(CHUNKS)]
+        o_codes = new([P, T], U32, "o_codes")
 
         def weave(c, copy, word):
             k, lo, hi = CHUNKS[c]
@@ -258,22 +259,29 @@ def tile_attend_gml_pl_nce_kernel(tc, xT, wd, wv, y, cw, rw, offs, out_0, out_1,
             src = pairs[k][:, :, lo - first : hi - first].rearrange("p u c e -> p u (c e)").bitcast(word)
             copy(woven[c][:].rearrange("p c u e -> p c (u e)").bitcast(word), src.rearrange("p u c -> p c u"))
 
+        STORED = {512: 0, 1024: 512, 1664: 1024, 2048: 1664}
+
         def emit(c):
             k, lo, hi = CHUNKS[c]
-            nc.vector.quantize_mx(out=o_codes[c][:].bitcast(E4M3), scales=o_scales[4 * (lo // 1024) :, lo % 1024 : lo % 1024 + hi - lo], in_=woven[c][:].rearrange("p c u e -> p (c u e)"))
-            nc.sync.dma_start(out=words_out[:, lo:hi], in_=o_codes[c][:].bitcast(I32))
+            nc.vector.quantize_mx(out=o_codes[:, lo:hi].bitcast(E4M3), scales=o_scales[4 * (lo // 1024) :, lo % 1024 : lo % 1024 + hi - lo], in_=woven[c][:].rearrange("p c u e -> p (c u e)"))
+            if hi in STORED:
+                nc.sync.dma_start(out=words_out[:, STORED[hi] : hi], in_=o_codes[:, STORED[hi] : hi].bitcast(I32))
 
-        nc.scalar.copy(*rounded(0, 1, *GROUPS[1]))
-        for c in (3, 4):
-            nc.scalar.copy(*rounded(1, *CHUNKS[c]))
-        for c in (3, 4):
+        nc.scalar.copy(*rounded(0, 0, MINE, T))
+        nc.scalar.copy(*rounded(1, *CHUNKS[3]))
+        nc.scalar.copy(*rounded(1, 0, 1664, T))
+        for c in (3, 4, 5):
             weave(c, nc.scalar.copy, U32)
-        nc.vector.tensor_copy(*rounded(0, 0, *GROUPS[0]))
-        nc.vector.tensor_copy(*rounded(1, 0, 0, 512))
-        nc.vector.tensor_copy(*rounded(1, 0, 512, 1280))
-        for c in range(3):
+        for t in range(2):
+            nc.vector.tensor_copy(*rounded(t, 0, 0, 512))
+        weave(0, nc.vector.tensor_copy, I32)
+        emit(0)
+        for t in range(2):
+            nc.vector.tensor_copy(*rounded(t, 0, 512, MINE))
+        for c in (1, 2):
             weave(c, nc.vector.tensor_copy, I32)
-        for c in range(len(CHUNKS)):
+            emit(c)
+        for c in (3, 4, 5):
             emit(c)
         scales_out = out_2.rearrange("o f c -> (o f) c").bitcast(I32).rearrange("f (h c) -> h f c", h=2)
         for q in range(4):

@@ -259,13 +259,12 @@ def tile_attend_gml_pl_nce_kernel(tc, xT, wd, wv, y, cw, rw, offs, out_0, out_1,
             src = pairs[k][:, :, lo - first : hi - first].rearrange("p u c e -> p u (c e)").bitcast(word)
             copy(woven[c][:].rearrange("p c u e -> p c (u e)").bitcast(word), src.rearrange("p u c -> p c u"))
 
-        STORED = {512: 0, 1024: 512, 1664: 1024, 2048: 1664}
-
         def emit(c):
             k, lo, hi = CHUNKS[c]
             nc.vector.quantize_mx(out=o_codes[:, lo:hi].bitcast(E4M3), scales=o_scales[4 * (lo // 1024) :, lo % 1024 : lo % 1024 + hi - lo], in_=woven[c][:].rearrange("p c u e -> p (c u e)"))
-            if hi in STORED:
-                nc.sync.dma_start(out=words_out[:, STORED[hi] : hi], in_=o_codes[:, STORED[hi] : hi].bitcast(I32))
+            if c != 4:
+                lo = CHUNKS[min(c, 4)][1]
+                nc.sync.dma_start(out=words_out[:, lo:hi], in_=o_codes[:, lo:hi].bitcast(I32))
 
         nc.scalar.copy(*rounded(0, 0, MINE, T))
         nc.scalar.copy(*rounded(1, *CHUNKS[3]))
@@ -278,10 +277,11 @@ def tile_attend_gml_pl_nce_kernel(tc, xT, wd, wv, y, cw, rw, offs, out_0, out_1,
         emit(0)
         for t in range(2):
             nc.vector.tensor_copy(*rounded(t, 0, 512, MINE))
-        for c in (1, 2):
-            weave(c, nc.vector.tensor_copy, I32)
-            emit(c)
-        for c in (3, 4, 5):
+        weave(1, nc.vector.tensor_copy, I32)
+        emit(1)
+        emit(3)
+        weave(2, nc.vector.tensor_copy, I32)
+        for c in (2, 4, 5):
             emit(c)
         scales_out = out_2.rearrange("o f c -> (o f) c").bitcast(I32).rearrange("f (h c) -> h f c", h=2)
         for q in range(4):

@@ -204,7 +204,9 @@ def tile_attend_gml_pl_nce_kernel(tc, xT, wd, wv, y, cw, rw, offs, out_0, out_1,
         GROUPS = [(0, T)]
         POOL, MINE = 1408, 1152
         pairs = [new([P, 2, T, 2], BF16, "pairs")]
-        dx = {(t, h): new([P, HALF], F32, "dx%d%d" % (t, h))[:] for t in range(4) for h in range(2) if (t, h) != (1, A)}
+        dx = {(t, h): new([P, HALF], F32, "dx%d%d" % (t, h))[:] for t, h in ((0, A), (0, B), (1, B), (2, A), (3, A))}
+        dx_late = new([P, 2, HALF], F32, "dx_late")
+        dx.update({(t, B): dx_late[:, t - 2] for t in (2, 3)})
         dx[1, A] = pairs[0][:, 1, T - HALF :].rearrange("p c e -> p (c e)").bitcast(F32)
 
         def scatter_early(t):
@@ -225,15 +227,21 @@ def tile_attend_gml_pl_nce_kernel(tc, xT, wd, wv, y, cw, rw, offs, out_0, out_1,
             scatter_early(t)
         quantize_g(1, B, 0, P)
         quantize_g(1, B, P, HALF)
-        late = {t: product(t, halves[B]) for t in (2, 3)}
+        third, fourth = slice(HALF, HALF + P), slice(HALF + P, N)
+        both = psum.tile([P, 2, P], F32, name="bank")
+        for g in range(2):
+            for e in range(2):
+                mx(both[:, e], wv_q[g, 1], e, g_q[g], third, E5M2, g + e == 0, g + e == 2)
+        late = {t: product(t, fourth) for t in (2, 3)}
         wv_q[1, 0] = quantize_pair(wv_d[1, 0], "wv10")
         for t in (0, 1):
             nc.scalar.copy(dx[t, A], product(t, halves[A])[:])
         for t in (0, 1):
             scatter_early(t)
             late[t] = product(t, halves[B])
+        nc.vector.tensor_copy(dx_late[:, :, :P], both[:])
         for t in (2, 3):
-            nc.vector.tensor_copy(dx[t, B], late[t][:])
+            nc.vector.tensor_copy(dx_late[:, t - 2, P:], late[t][:])
         scatter_late(2)
         store(2)
         for t in (0, 1):

@@ -202,12 +202,12 @@ def tile_attend_gml_pl_nce_kernel(tc, xT, wd, wv, y, cw, rw, offs, out_0, out_1,
 
         out_rows = out_0.rearrange("(p t) c -> t p c", t=4)
         GROUPS = [(0, T)]
-        POOL, MINE = 1408, 1152
+        POOL, MINE = T - 1408, T - 1152
         pairs = [new([P, 2, T, 2], BF16, "pairs")]
         dx = {(t, h): new([P, HALF], F32, "dx%d%d" % (t, h))[:] for t, h in ((0, A), (0, B), (1, B), (2, A), (3, A))}
         dx_late = new([P, 2, HALF], F32, "dx_late")
         dx.update({(t, B): dx_late[:, t - 2] for t in (2, 3)})
-        dx[1, A] = pairs[0][:, 1, T - HALF :].rearrange("p c e -> p (c e)").bitcast(F32)
+        dx[1, A] = pairs[0][:, 1, :HALF].rearrange("p c e -> p (c e)").bitcast(F32)
 
         def scatter_early(t):
             nc.scalar.activation(o_win[t][:].indirect(offsets[:, half_offsets[A]]), dx[t, A], ACT.Copy)
@@ -250,11 +250,11 @@ def tile_attend_gml_pl_nce_kernel(tc, xT, wd, wv, y, cw, rw, offs, out_0, out_1,
             scatter_late(t)
             store(t)
         for t in (2, 3):
-            nc.gpsimd.tensor_scalar(*rounded(t, 0, 0, POOL), 1.0, -0.0, ALU.mult, ALU.add)
+            nc.gpsimd.tensor_scalar(*rounded(t, 0, POOL, T), 1.0, -0.0, ALU.mult, ALU.add)
         for t in (2, 3):
-            nc.scalar.copy(*rounded(t, 0, POOL, T))
+            nc.scalar.copy(*rounded(t, 0, 0, POOL))
 
-        CHUNKS = [(0, 0, 512), (0, 512, 1024), (0, 1024, 1152), (0, 1152, 1664), (0, 1664, 1920), (0, 1920, 2048)]
+        CHUNKS = [(0, 1536, 2048), (0, 1024, 1536), (0, 896, 1024), (0, 0, 512), (0, 512, 768), (0, 768, 896)]
         reuse = ["x_win0", "x_win1", "x_win2", "x_win3", "wd_raw1", "wv_raw0"]
         woven = [new([P, hi - lo, 2, 2], BF16, "woven%d" % c, tag=reuse[c]) for c, (k, lo, hi) in enumerate(CHUNKS)]
         words_out = out_1.rearrange("o p c l -> p (o c l)").bitcast(I32)
@@ -270,21 +270,21 @@ def tile_attend_gml_pl_nce_kernel(tc, xT, wd, wv, y, cw, rw, offs, out_0, out_1,
         def emit(c):
             k, lo, hi = CHUNKS[c]
             nc.vector.quantize_mx(out=o_codes[:, lo:hi].bitcast(E4M3), scales=o_scales[4 * (lo // 1024) :, lo % 1024 : lo % 1024 + hi - lo], in_=woven[c][:].rearrange("p c u e -> p (c u e)"))
-            if c != 4:
-                lo = CHUNKS[min(c, 4)][1]
+            if c != 2:
+                hi = CHUNKS[2][2] if c == 5 else hi
                 nc.sync.dma_start(out=words_out[:, lo:hi], in_=o_codes[:, lo:hi].bitcast(I32))
 
-        nc.scalar.copy(*rounded(0, 0, MINE, T))
+        nc.scalar.copy(*rounded(0, 0, 0, MINE))
         nc.scalar.copy(*rounded(1, *CHUNKS[3]))
-        nc.scalar.copy(*rounded(1, 0, 1664, T))
+        nc.scalar.copy(*rounded(1, 0, 512, MINE))
         for c in (3, 4, 5):
             weave(c, nc.scalar.copy, U32)
         for t in range(2):
-            nc.vector.tensor_copy(*rounded(t, 0, 0, 512))
+            nc.vector.tensor_copy(*rounded(t, *CHUNKS[0]))
         weave(0, nc.vector.tensor_copy, I32)
         emit(0)
         for t in range(2):
-            nc.vector.tensor_copy(*rounded(t, 0, 512, MINE))
+            nc.vector.tensor_copy(*rounded(t, 0, MINE, 1536))
         weave(1, nc.vector.tensor_copy, I32)
         emit(1)
         emit(3)

@@ -60,10 +60,12 @@ def tile_attend_gml_pl_nce_kernel(tc, xT, wd, wv, y, cw, rw, offs, out_0, out_1,
             nc.sync.dma_start(out=wd_raw[0][h][:], in_=wd_rows[:, :, 256 * h : 256 * (h + 1)])
         load_y(0, A)
         nc.sync.dma_start(out=wd_raw[1][0][:], in_=wd_rows[:, :, 512:])
-        load_y(0, B)
+        for lanes in (slice(0, 2), slice(2, 4)):
+            nc.sync.dma_start(out=y_sb[0, B][:, lanes], in_=y_rows[0][:, lanes, halves[B]])
         nc.sync.dma_start(out=wv_raw[0][0][:], in_=wv_rows[0])
         load_y(1, A)
-        nc.sync.dma_start(out=wv_raw[1][0][:], in_=wv_rows[1])
+        for h in range(2):
+            nc.sync.dma_start(out=wv_raw[1][0][:, :, halves[h]], in_=wv_rows[1][:, :, halves[h]])
         for lanes in (slice(0, 2), slice(2, 4)):
             nc.sync.dma_start(out=y_sb[1, B][:, lanes], in_=y_rows[1][:, lanes, halves[B]])
 
@@ -101,10 +103,10 @@ def tile_attend_gml_pl_nce_kernel(tc, xT, wd, wv, y, cw, rw, offs, out_0, out_1,
         for h in range(2):
             quantize(x_q[h], slice(0, HALF), x_g[:, halves[h]].rearrange("p n t -> p (n t)"), E4M3)
 
-        def deal(dealt, raw, k, piece, copy):
+        def deal(dealt, raw, k, piece, copy, part=slice(None)):
             rows = P // len(raw)
             src = raw[piece][:].rearrange("p j (m t) -> p m j t", t=4)[:, :, :, 2 * k : 2 * k + 2]
-            copy(dealt[:].rearrange("p t m j -> p m j t")[:, rows * piece : rows * (piece + 1)], src)
+            copy(dealt[:].rearrange("p t m j -> p m j t")[:, rows * piece : rows * (piece + 1)][:, part], src[:, part])
 
         def dealt_tile(name, tag=None):
             return new([P, 2, P, 4], BF16, name, tag)
@@ -166,7 +168,8 @@ def tile_attend_gml_pl_nce_kernel(tc, xT, wd, wv, y, cw, rw, offs, out_0, out_1,
         for k in range(2):
             deal(wd1[k], wd_raw[1], k, 0, nc.scalar.copy)
         weigh(0, A)
-        subtract(0, B, slice(0, 4))
+        for lanes in (low, high):
+            subtract(0, B, lanes)
         wd1_q = [quantize_pair(wd1[0], "wd10")]
         weigh(0, B)
         wd1_q.append(quantize_pair(wd1[1], "wd11"))
@@ -177,7 +180,8 @@ def tile_attend_gml_pl_nce_kernel(tc, xT, wd, wv, y, cw, rw, offs, out_0, out_1,
         scores(wd1_q, 1, A, low)
         scores(wd1_q, 1, A, high)
         deal(wv_d[0, 1], wv_raw[0], 1, 0, nc.scalar.copy)
-        deal(wv_d[1, 1], wv_raw[1], 1, 0, nc.scalar.copy)
+        for h in range(2):
+            deal(wv_d[1, 1], wv_raw[1], 1, 0, nc.scalar.copy, slice(P // 2 * h, P // 2 * (h + 1)))
         for lanes in (low, high):
             scores(wd1_q, 1, B, lanes)
         deal(wv_d[1, 0], wv_raw[1], 0, 0, nc.scalar.copy)

from contextlib import ExitStack

import concourse.mybir as mybir
from concourse.masks import make_identity

N, T, D, V = 512, 2048, 512, 1024
FLOPS = 2 * 2 * D * V * N

F32 = mybir.dt.float32
BF16 = mybir.dt.bfloat16
I32 = mybir.dt.int32
U32 = mybir.dt.uint32
U16 = mybir.dt.uint16
U8 = mybir.dt.uint8
E4M3 = mybir.dt.float8_e4m3fn_x4
E5M2 = mybir.dt.float8_e5m2_x4
ACT = mybir.ActivationFunctionType
ALU = mybir.AluOpType

P = 128
HALF = N // 2
A, B = 0, 1


def tile_attend_gml_pl_nce_kernel(tc, xT, wd, wv, y, cw, rw, offs, out_0, out_1, out_2):
    nc = tc.nc
    with ExitStack() as ctx:
        lists = ctx.enter_context(tc.tile_pool(name="lists", bufs=1))
        sb = ctx.enter_context(tc.tile_pool(name="sb", bufs=1))
        psum = ctx.enter_context(tc.psum_pool(name="psum", bufs=8))

        def new(shape, dtype, name, tag=None):
            return sb.tile(shape, dtype, name=name, tag=tag or name, align_bytes=64)

        halves = [slice(0, HALF), slice(HALF, N)]
        half_offsets = [slice(0, HALF // 16), slice(HALF // 16, N // 16)]

        x_rows = xT.rearrange("(p t) c -> t p c", t=4)
        x_win = [new([P, T], F32, "x_win%d" % t) for t in range(4)]
        offsets = lists.tile([P, N // 16], U16, name="offsets")
        cw_sb = new([P, 2, 4], F32, "cw_sb")
        rw_sb = new([P, 4], F32, "rw_sb")
        wd_raw = [[new([P, 4, 256], F32, "wd_raw0%d" % h) for h in range(2)], [new([P, 4, 512], F32, "wd_raw1")]]
        wv_raw = [[new([P, 4, 512], F32, "wv_raw%d" % g)] for g in range(2)]
        y_sb = {(g, h): new([P, 4, HALF], F32, "y%d%d" % (g, h)) for g in range(2) for h in range(2)}
        wd_rows = wd.rearrange("(p j) v -> p j v", j=4)
        wv_rows = wv.rearrange("(g p j) d -> g p j d", g=2, j=4)
        y_rows = y.rearrange("(g p t) i -> g p t i", g=2, t=4)

        def load_y(g, h):
            nc.sync.dma_start(out=y_sb[g, h][:], in_=y_rows[g][:, :, halves[h]])

        nc.sync.dma_start(out=x_win[0][:], in_=x_rows[0])
        nc.sync.dma_start(offsets[:], offs)
        nc.scalar.dma_start(out=cw_sb[:], in_=cw.rearrange("(g p t) o -> p g (t o)", g=2, t=4))
        nc.scalar.dma_start(out=rw_sb[:], in_=rw[0:1, :].rearrange("o (p c) -> (o p) c", c=4))
        for t in range(1, 4):
            nc.sync.dma_start(out=x_win[t][:], in_=x_rows[t])
        for h in range(2):
            nc.sync.dma_start(out=wd_raw[0][h][:], in_=wd_rows[:, :, 256 * h : 256 * (h + 1)])
        load_y(0, A)
        nc.sync.dma_start(out=wd_raw[1][0][:], in_=wd_rows[:, :, 512:])
        for lanes in (slice(0, 2), slice(2, 4)):
            nc.sync.dma_start(out=y_sb[0, B][:, lanes], in_=y_rows[0][:, lanes, halves[B]])
        nc.sync.dma_start(out=wv_raw[0][0][:], in_=wv_rows[0])
        load_y(1, A)
        for h in range(2):
            nc.sync.dma_start(out=wv_raw[1][0][:, :, halves[h]], in_=wv_rows[1][:, :, halves[h]])
        for lanes in (slice(0, 2), slice(2, 4)):
            nc.sync.dma_start(out=y_sb[1, B][:, lanes], in_=y_rows[1][:, lanes, halves[B]])

        warm = new([P, 8], F32, "warm")
        nc.vector.memset(warm[:, 0:1], 0.0)
        nc.scalar.activation(warm[:, 1:2], warm[:, 0:1], ACT.Sigmoid)
        o_win = [new([P, T], F32, "o_win%d" % t) for t in range(4)]
        for t in range(2):
            nc.vector.memset(o_win[t][:].bitcast(I32), 0)
        ident = new([P, P], F32, "ident")
        make_identity(nc, ident[:])
        for t in range(2, 4):
            nc.gpsimd.memset(o_win[t][:].bitcast(I32), 0)
        rw_bank = psum.tile([P, 4, P], F32, name="bank")
        for c in range(4):
            nc.tensor.transpose(rw_bank[:, c, :], rw_sb[:, c : c + 1].to_broadcast([P, P]), ident[:])
        rw_all = rw_bank[:].rearrange("p c n -> p n c")
        w_sb = [new([P, N // 4, 4, 4], F32, "w_sb%d" % g) for g in range(2)]
        for g in range(2):
            for t in range(4):
                nc.scalar.activation(w_sb[g][:, :, t, :], rw_all, ACT.Copy, scale=cw_sb[:, g, t : t + 1])

        def operand(width, name, tag=None):
            return new([P, width], U32, name + "_codes", tag), new([P, width], U8, name + "_scales")

        def quantize(dst, cols, grouped, fmt):
            nc.vector.quantize_mx(out=dst[0][:, cols].bitcast(fmt), scales=dst[1][:, cols], in_=grouped)

        x_g = new([P, N, 4], BF16, "x_g")
        for t in range(3):
            nc.vector.tensor_copy(x_g[:, :, t], x_win[t][:].indirect(offsets[:]))
        for h in range(2):
            nc.vector.tensor_copy(x_g[:, halves[h], 3], x_win[3][:].indirect(offsets[:, half_offsets[h]]))
        x_q = [operand(HALF, "x%d" % h) for h in range(2)]
        for h in range(2):
            quantize(x_q[h], slice(0, HALF), x_g[:, halves[h]].rearrange("p n t -> p (n t)"), E4M3)

        def deal(dealt, raw, k, piece, copy, part=slice(None)):
            rows = P // len(raw)
            src = raw[piece][:].rearrange("p j (m t) -> p m j t", t=4)[:, :, :, 2 * k : 2 * k + 2]
            copy(dealt[:].rearrange("p t m j -> p m j t")[:, rows * piece : rows * (piece + 1)][:, part], src[:, part])

        def dealt_tile(name, tag=None):
            return new([P, 2, P, 4], BF16, name, tag)

        def quantize_pair(dealt, name):
            q = operand(2 * P, name)
            quantize(q, slice(0, 2 * P), dealt[:].rearrange("p t m j -> p (t m j)"), E4M3)
            return q

        def mx(out, lhs, e, rhs, cols, fmt, start, stop):
            lane = slice(P * e, P * (e + 1))
            nc.tensor.matmul_mx(out=out, lhsT=lhs[0][:, lane].bitcast(E4M3), lhsT_scale=lhs[1][:, lane], rhs=rhs[0][:, cols].bitcast(fmt), rhs_scale=rhs[1][:, cols], start=start, stop=stop)

        s_sb = {(g, h): new([P, 4, HALF], F32, "s%d%d" % (g, h)) for g in range(2) for h in range(2)}
        grad0 = new([P, N, 4], BF16, "grad0")
        grad = {(0, h): grad0[:, halves[h]] for h in range(2)}
        grad.update({(1, h): new([P, HALF, 4], BF16, "grad1%d" % h)[:] for h in range(2)})
        g_q = [operand(N, "g%d" % g) for g in range(2)]

        def scores(wd_q, g, h, lanes):
            bank = psum.tile([P, lanes.stop - lanes.start, HALF], F32, name="bank")
            for t in range(lanes.start, lanes.stop):
                mx(bank[:, t - lanes.start], wd_q[t // 2], t % 2, x_q[h], slice(0, HALF), E4M3, True, True)
            nc.scalar.activation(s_sb[g, h][:, lanes], bank[:], ACT.Sigmoid)

        def subtract(g, h, lanes):
            nc.vector.tensor_tensor(y_sb[g, h][:, lanes], s_sb[g, h][:, lanes], y_sb[g, h][:, lanes], ALU.subtract)

        def weigh(g, h, lo=0, hi=HALF):
            nc.vector.tensor_tensor(
                grad[g, h][:, lo:hi].rearrange("p (c i) t -> p c t i", i=4),
                y_sb[g, h][:, :, lo:hi].rearrange("p t (c i) -> p c t i", i=4),
                w_sb[g][:, (HALF * h + lo) // 4 : (HALF * h + hi) // 4],
                ALU.mult,
            )

        def quantize_g(g, h, lo=0, hi=HALF):
            quantize(g_q[g], slice(HALF * h + lo, HALF * h + hi), grad[g, h][:, lo:hi].rearrange("p n t -> p (n t)"), E5M2)

        low, high = slice(0, 2), slice(2, 4)

        wd0 = [dealt_tile("wd0%d" % k) for k in range(2)]
        deal(wd0[0], wd_raw[0], 0, 0, nc.scalar.copy)
        deal(wd0[1], wd_raw[0], 1, 0, nc.scalar.copy)
        deal(wd0[0], wd_raw[0], 0, 1, nc.vector.tensor_copy)
        deal(wd0[1], wd_raw[0], 1, 1, nc.scalar.copy)
        wd0_q = [operand(2 * P, "wd00")]
        for e in range(2):
            quantize(wd0_q[0], slice(P * e, P * (e + 1)), wd0[0][:, e].rearrange("p m j -> p (m j)"), E4M3)
        wd0_q.append(quantize_pair(wd0[1], "wd01"))
        single = [slice(t, t + 1) for t in range(4)]
        for lanes in single:
            scores(wd0_q, 0, A, lanes)
        for lanes in (low, high):
            scores(wd0_q, 0, B, lanes)
        for lanes in single:
            subtract(0, A, lanes)
        wd1 = [dealt_tile("wd1%d" % k) for k in range(2)]
        for k in range(2):
            deal(wd1[k], wd_raw[1], k, 0, nc.scalar.copy)
        weigh(0, A)
        for lanes in (low, high):
            subtract(0, B, lanes)
        wd1_q = [quantize_pair(wd1[0], "wd10")]
        weigh(0, B)
        wd1_q.append(quantize_pair(wd1[1], "wd11"))
        quantize(g_q[0], slice(0, N), grad0[:].rearrange("p n t -> p (n t)"), E5M2)

        wv_d = {(g, k): dealt_tile("wv%d%d" % (g, k)) for g in range(2) for k in range(2)}
        wv_q = {}
        scores(wd1_q, 1, A, low)
        scores(wd1_q, 1, A, high)
        deal(wv_d[0, 1], wv_raw[0], 1, 0, nc.scalar.copy)
        for h in range(2):
            deal(wv_d[1, 1], wv_raw[1], 1, 0, nc.scalar.copy, slice(P // 2 * h, P // 2 * (h + 1)))
        for lanes in (low, high):
            scores(wd1_q, 1, B, lanes)
        deal(wv_d[1, 0], wv_raw[1], 0, 0, nc.scalar.copy)
        subtract(1, A, low)
        subtract(1, A, high)
        deal(wv_d[0, 0], wv_raw[0], 0, 0, nc.vector.tensor_copy)
        wv_q[0, 1] = quantize_pair(wv_d[0, 1], "wv01")
        weigh(1, A)
        subtract(1, B, low)
        wv_q[1, 1] = quantize_pair(wv_d[1, 1], "wv11")
        quantize_g(1, A)
        subtract(1, B, high)
        wv_q[0, 0] = quantize_pair(wv_d[0, 0], "wv00")
        weigh(1, B, 0, P)
        weigh(1, B, P, HALF)

        def product(t, cols):
            bank = psum.tile([P, cols.stop - cols.start], F32, name="bank")
            for g in range(2):
                mx(bank[:], wv_q[g, t // 2], t % 2, g_q[g], cols, E5M2, g == 0, g == 1)
            return bank

        out_rows = out_0.rearrange("(p t) c -> t p c", t=4)
        GROUPS = [(0, T)]
        POOL, MINE = T - 1408, T - 1152
        pairs = [new([P, 2, T, 2], BF16, "pairs")]
        dx = {(t, h): new([P, HALF], F32, "dx%d%d" % (t, h))[:] for t, h in ((0, A), (0, B), (1, B), (2, A), (3, A))}
        dx_late = new([P, 2, HALF], F32, "dx_late")
        dx.update({(t, B): dx_late[:, t - 2] for t in (2, 3)})
        dx[1, A] = pairs[0][:, 1, :HALF].rearrange("p c e -> p (c e)").bitcast(F32)

        def scatter_early(t):
            nc.scalar.activation(o_win[t][:].indirect(offsets[:, half_offsets[A]]), dx[t, A], ACT.Copy)

        def scatter_late(t):
            nc.vector.tensor_copy(o_win[t][:].indirect(offsets[:, half_offsets[B]]), dx[t, B])

        def store(t):
            nc.sync.dma_start(out=out_rows[t], in_=o_win[t][:])

        def rounded(t, k, lo, hi):
            first = GROUPS[k][0]
            return pairs[k][:, t // 2, lo - first : hi - first, t % 2], o_win[t][:, lo:hi]

        for t in (2, 3):
            nc.scalar.copy(dx[t, A], product(t, halves[A])[:])
            scatter_early(t)
        quantize_g(1, B, 0, P)
        quantize_g(1, B, P, HALF)
        third, fourth = slice(HALF, HALF + P), slice(HALF + P, N)
        both = psum.tile([P, 2, P], F32, name="bank")
        for g in range(2):
            for e in range(2):
                mx(both[:, e], wv_q[g, 1], e, g_q[g], third, E5M2, g + e == 0, g + e == 2)
        late = {t: product(t, fourth) for t in (2, 3)}
        wv_q[1, 0] = quantize_pair(wv_d[1, 0], "wv10")
        for t in (0, 1):
            nc.scalar.copy(dx[t, A], product(t, halves[A])[:])
        for t in (0, 1):
            scatter_early(t)
            late[t] = product(t, halves[B])
        nc.vector.tensor_copy(dx_late[:, :, :P], both[:])
        for t in (2, 3):
            nc.vector.tensor_copy(dx_late[:, t - 2, P:], late[t][:])
        scatter_late(2)
        store(2)
        for t in (0, 1):
            nc.vector.tensor_copy(dx[t, B], late[t][:])
        for t in (3, 0, 1):
            scatter_late(t)
            store(t)
        for t in (2, 3):
            nc.gpsimd.tensor_scalar(*rounded(t, 0, POOL, T), 1.0, -0.0, ALU.mult, ALU.add)
        for t in (2, 3):
            nc.scalar.copy(*rounded(t, 0, 0, POOL))

        CHUNKS = [(0, 1536, 2048), (0, 1024, 1536), (0, 896, 1024), (0, 0, 512), (0, 512, 768), (0, 768, 896)]
        reuse = ["x_win0", "x_win1", "x_win2", "x_win3", "wd_raw1", "wv_raw0"]
        woven = [new([P, hi - lo, 2, 2], BF16, "woven%d" % c, tag=reuse[c]) for c, (k, lo, hi) in enumerate(CHUNKS)]
        words_out = out_1.rearrange("o p c l -> p (o c l)").bitcast(I32)
        o_scales = new([P, T // 2], U8, "o_scales")
        o_codes = new([P, T], U32, "o_codes")

        def weave(c, copy, word):
            k, lo, hi = CHUNKS[c]
            first = GROUPS[k][0]
            src = pairs[k][:, :, lo - first : hi - first].rearrange("p u c e -> p u (c e)").bitcast(word)
            copy(woven[c][:].rearrange("p c u e -> p c (u e)").bitcast(word), src.rearrange("p u c -> p c u"))

        def emit(c):
            k, lo, hi = CHUNKS[c]
            nc.vector.quantize_mx(out=o_codes[:, lo:hi].bitcast(E4M3), scales=o_scales[4 * (lo // 1024) :, lo % 1024 : lo % 1024 + hi - lo], in_=woven[c][:].rearrange("p c u e -> p (c u e)"))
            if c != 2:
                hi = CHUNKS[2][2] if c == 5 else hi
                nc.sync.dma_start(out=words_out[:, lo:hi], in_=o_codes[:, lo:hi].bitcast(I32))

        nc.scalar.copy(*rounded(0, 0, 0, MINE))
        nc.scalar.copy(*rounded(1, *CHUNKS[3]))
        nc.scalar.copy(*rounded(1, 0, 512, MINE))
        for c in (3, 4, 5):
            weave(c, nc.scalar.copy, U32)
        for t in range(2):
            nc.vector.tensor_copy(*rounded(t, *CHUNKS[0]))
        weave(0, nc.vector.tensor_copy, I32)
        emit(0)
        for t in range(2):
            nc.vector.tensor_copy(*rounded(t, 0, MINE, 1536))
        weave(1, nc.vector.tensor_copy, I32)
        emit(1)
        emit(3)
        weave(2, nc.vector.tensor_copy, I32)
        for c in (2, 4, 5):
            emit(c)
        scales_out = out_2.rearrange("o f c -> (o f) c").bitcast(I32).rearrange("f (h c) -> h f c", h=2)
        for q in range(4):
            nc.sync.dma_start(out=scales_out[:, 4 * q : 4 * q + 4, :], in_=o_scales[32 * q : 32 * q + 8, :].bitcast(I32))
